import numpy as np
import ml_dtypes


def mxq(x, axis, fmt="e4m3"):
    dtype, down = {"e4m3": (ml_dtypes.float8_e4m3fn, 7), "e5m2": (ml_dtypes.float8_e5m2, 14)}[fmt]
    v = np.moveaxis(np.asarray(x, np.float32).astype(ml_dtypes.bfloat16).astype(np.float64), axis, -1)
    blocks = v.reshape(v.shape[:-1] + (-1, 32))
    amax = np.abs(blocks).max(-1, keepdims=True)
    byte = np.maximum(np.where(amax > 0, np.frexp(amax)[1] - 1 + 127, 0) - down, 1)
    scale = np.exp2(byte - 127.0)
    codes = (blocks / scale).astype(np.float32).astype(dtype).astype(np.float64)
    return np.moveaxis((codes * scale).reshape(v.shape), -1, axis)


WIDE = False


def mx_kscale(k):
    if not WIDE:
        return np.ones(k)
    levels = np.array([10, -10, 5, -5, 0])
    if k % 512:
        return np.exp2(np.random.permutation(np.resize(levels, k // 32))).repeat(32)
    a = np.empty((k // 512, 16))
    for p in range(k // 512):
        a[p, :8] = np.random.permutation(np.resize(levels, 8))
        for g in range(8):
            far = levels[np.abs(levels - a[p, g]) >= 10]
            a[p, g + 8] = far[np.random.randint(len(far))]
    return np.exp2(a.ravel()).repeat(32)


BF16 = ml_dtypes.bfloat16


def bf(x):
    return np.asarray(x, np.float32).astype(BF16)


def f64(x):
    return np.asarray(x).astype(np.float64)


N = 1024


def draw0():
    s = mx_kscale(N)
    return {"f": bf(np.random.standard_normal((N, N)) * s[:, None] * s),
            "x": bf(np.random.standard_normal((N, N)) / np.sqrt(N) / s[:, None]),
            "y": bf(np.random.standard_normal((N, N)) * s[:, None]),
            "v": bf(0.5 * np.random.standard_normal(N))}


def core(f, x, y, v):
    xq = mxq(f64(x), 0, "e4m3")
    half = mxq(f64(f), 1, "e4m3") @ xq
    half = half + f64(v)[:, None] * f64(y)
    return xq.T @ mxq(half, 0, "e4m3")


def e4m3fn_bytes(y):
    return np.clip(np.asarray(y, np.float64), -448.0, 448.0).astype(np.float32).astype(ml_dtypes.float8_e4m3fn).view(np.uint8)


def e4m3fn_values(b):
    return np.asarray(b, np.uint8).view(ml_dtypes.float8_e4m3fn).astype(np.float64)


def setup_inputs():
    d = draw0()
    x0 = np.asarray(d['x']).astype(np.float64)
    s = (np.max(np.abs(x0), axis=(1,), keepdims=True) / 448.0).astype(np.float32)
    out = {}
    for k, v in d.items():
        if k == 'x':
            out['x_bytes'] = e4m3fn_bytes(x0 / s.astype(np.float64))
            out['x_scale'] = s
        else:
            out[k] = v
    return out


def reference(f, x_bytes, x_scale, y, v):
    return core(f, e4m3fn_values(x_bytes) * x_scale.astype(np.float64), y, v)

@@ -1,0 +1,406 @@
+from contextlib import ExitStack
+
+import concourse.mybir as mybir
+from concourse.masks import make_identity
+
+N = 1024
+FLOPS = 2 * 2 * N * N * N
+
+F32 = mybir.dt.float32
+BF16 = mybir.dt.bfloat16
+U32 = mybir.dt.uint32
+U8 = mybir.dt.uint8
+FP8 = mybir.dt.float8_e4m3fn
+FP8X4 = mybir.dt.float8_e4m3fn_x4
+COPY = mybir.ActivationFunctionType.Copy
+MULT = mybir.AluOpType.mult
+ADD = mybir.AluOpType.add
+
+P = 128
+G = 2
+T = 4
+Q = 256
+H = 512
+
+
+def tile_loewdin_fock_shift_s7_kernel(tc, f, x_bytes, x_scale, y, v, out):
+    nc = tc.nc
+    x_rows = x_bytes.rearrange("(g p t) j -> g p t j", p=P, t=T)
+    f_rows = f.rearrange("(g p t) b -> g p t b", p=P, t=T)
+    y_rows = y.rearrange("(g p t) j -> g p t j", p=P, t=T)
+
+    with ExitStack() as ctx:
+        keep = ctx.enter_context(tc.tile_pool(name="keep", bufs=1))
+        psum = ctx.enter_context(tc.psum_pool(name="psum", bufs=4))
+        ctx.enter_context(tc.manual_schedule())
+
+        def grid(name, rows, cols, shape, dtype):
+            return [
+                [keep.tile(shape, dtype, name="%s_%d_%d" % (name, a, b), align_bytes=64) for b in range(cols)]
+                for a in range(rows)
+            ]
+
+        xs = keep.tile([P, G * T], F32, name="xs")
+        vb = keep.tile([P, G * T], BF16, name="vb")
+        vf = keep.tile([P, G * T], F32, name="vf")
+        ident = keep.tile([P, P], F32, name="ident")
+        warm = keep.tile([P, 2], F32, name="warm")
+        dz = keep.tile([P, H], BF16, name="dz", align_bytes=64)
+        xb = grid("xb", G, 2, [P, T, H], U8)
+        xw = grid("xw", G, 4, [P, T, Q], BF16)
+        xi = grid("xi", G, 4, [P, Q, T], BF16)
+        xc = grid("xc", G, 4, [P, Q], U32)
+        xk = grid("xk", G, 4, [P, Q], U8)
+        fs = grid("fs", G, 2, [P, 2, N], BF16)
+        fi = grid("fi", G, 2, [P, 2, G * P * T], BF16)
+        fc = grid("fc", G, 2, [P, 2 * G * P], U32)
+        fk = grid("fk", G, 2, [P, 2 * G * P], U8)
+        ys = grid("ys", G, 2, [P, T, H], BF16)
+        vy = grid("vy", G, 2, [P, T, H], F32)
+        hi = grid("hi", G, 4, [P, Q, T], BF16)
+        hc = grid("hc", G, 4, [P, Q], U32)
+        hk = grid("hk", G, 4, [P, Q], U8)
+        os_ = grid("os", 4, 4, [P, 2, Q], F32)
+
+        nc.scalar.dma_start(out=xs[:], in_=x_scale.rearrange("(g p t) o -> p g (t o)", p=P, t=T))
+        nc.scalar.dma_start(out=vb[:], in_=v.rearrange("(g p t) -> p g t", p=P, t=T))
+        nc.sync.dma_start(out=xb[0][0][:], in_=x_rows[0][:, :, 0*H:0*H+H])
+        nc.sync.dma_start(out=xb[1][0][:], in_=x_rows[1][:, :, 0*H:0*H+H])
+        nc.sync.dma_start(out=fs[1][1][:], in_=f_rows[1][:, 2:4, :])
+        nc.sync.dma_start(out=fs[0][1][:], in_=f_rows[0][:, 2:4, :])
+        nc.sync.dma_start(out=fs[0][0][:], in_=f_rows[0][:, 0:2, :])
+        nc.sync.dma_start(out=fs[1][0][:], in_=f_rows[1][:, 0:2, :])
+        nc.sync.dma_start(out=ys[0][0][:], in_=y_rows[0][:, :, 0*H:0*H+H])
+        nc.sync.dma_start(out=ys[1][0][:], in_=y_rows[1][:, :, 0*H:0*H+H])
+        nc.sync.dma_start(out=xb[1][1][:], in_=x_rows[1][:, :, 1*H:1*H+H])
+        nc.sync.dma_start(out=xb[0][1][:], in_=x_rows[0][:, :, 1*H:1*H+H])
+        nc.sync.dma_start(out=ys[0][1][:], in_=y_rows[0][:, :, 1*H:1*H+H])
+        nc.sync.dma_start(out=ys[1][1][:], in_=y_rows[1][:, :, 1*H:1*H+H])
+
+        nc.vector.memset(dz[:], 0.0)
+        nc.vector.memset(warm[:], 0.0)
+        nc.scalar.activation(out=warm[:, 1:2], in_=warm[:, 0:1], func=COPY)
+        make_identity(nc, ident[:])
+
+        cv = nc.vector.tensor_copy
+        cs = nc.scalar.copy
+
+        def widen(g, q, t, eng):
+            (widen_v if eng == "V" else widen_s)(g, q, t)
+
+        def widen_s(g, q, t):
+            src = xb[g][q // 2][:, t, (q % 2) * Q : (q % 2 + 1) * Q].bitcast(FP8)
+            nc.scalar.activation(out=xw[g][q][:, t, :], in_=src, func=COPY, scale=xs[:, g * T + t : g * T + t + 1])
+
+        def widen_v(g, q, t):
+            src = xb[g][q // 2][:, t, (q % 2) * Q : (q % 2 + 1) * Q].bitcast(FP8)
+            nc.vector.tensor_scalar(
+                out=xw[g][q][:, t, :], in0=src, scalar1=xs[:, g * T + t : g * T + t + 1], scalar2=None, op0=MULT
+            )
+
+        def lay(g, q, eng):
+            (nc.vector.tensor_copy if eng == "V" else nc.scalar.copy)(
+                out=xi[g][q][:].rearrange("p (c i) t -> p c t i", i=4),
+                in_=xw[g][q][:].rearrange("p t (c i) -> p c t i", i=4),
+            )
+
+        def quant_x(g, q):
+            nc.vector.quantize_mx(
+                out=xc[g][q][:].bitcast(FP8X4), scales=xk[g][q][:], in_=xi[g][q][:].rearrange("p j t -> p (j t)")
+            )
+
+        tps = {}
+
+        def turn(g, t):
+            ps = psum.tile([P, G, 2, P], F32, name="work_ps", tag="work")
+            words = fs[g][t // 2][:, t % 2, :].bitcast(F32)
+            for c in range(G):
+                for u in range(2):
+                    nc.tensor.transpose(ps[:, c, u, :], words[:, 256 * c + u : 256 * (c + 1) : 2], ident[:])
+            tps[(g, t)] = ps
+
+        def turn_out(g, t, e):
+            eng = {"V": cv, "S": cs}[e]
+            dst = fi[g][t // 2][:, t % 2, :].bitcast(F32).rearrange("p (c r u) -> p c r u", c=G, u=2)
+            eng(out=dst, in_=tps[(g, t)][:].rearrange("p c u r -> p c r u"))
+
+        def quant_f(g, r):
+            nc.vector.quantize_mx(
+                out=fc[g][r][:].bitcast(FP8X4), scales=fk[g][r][:], in_=fi[g][r][:].rearrange("p s k -> p (s k)")
+            )
+
+        def shift(g, h, t, eng):
+            src = ys[g][h][:, t, :]
+            dst = vy[g][h][:, t, :]
+            col = vf[:, g * T + t : g * T + t + 1]
+            if eng == "S":
+                nc.scalar.activation(out=dst, in_=src, func=COPY, scale=col)
+            elif eng == "V":
+                nc.vector.tensor_scalar(out=dst, in0=src, scalar1=col, scalar2=None, op0=MULT)
+            else:
+                nc.gpsimd.tensor_scalar(out=dst, in0=src, scalar1=col, scalar2=0.0, op0=MULT, op1=ADD)
+
+        spin = psum.tile([P, H], F32, name="spin_ps", tag="half")
+
+        def keep_warm(count):
+            for k in range(count):
+                nc.tensor.matmul(spin[:], lhsT=dz[:, 0:P], rhs=dz[:], start=True, stop=True)
+
+        gps = {}
+
+        def first(g, q, n):
+            ps = psum.tile([P, T, P], F32, name="half_ps", tag="half")
+            cols = slice(n * P, (n + 1) * P)
+            for t in range(T):
+                for c in range(G):
+                    w = slice((t % 2) * 2 * P + c * P, (t % 2) * 2 * P + (c + 1) * P)
+                    nc.tensor.matmul_mx(
+                        out=ps[:, t, :],
+                        lhsT=fc[g][t // 2][:, w].bitcast(FP8X4),
+                        lhsT_scale=fk[g][t // 2][:, w],
+                        rhs=xc[c][q][:, cols].bitcast(FP8X4),
+                        rhs_scale=xk[c][q][:, cols],
+                        start=(c == 0),
+                        stop=(c == G - 1),
+                    )
+            gps[(g, q, n)] = ps
+
+        def shifted(g, q, n):
+            j0 = (q % 2) * Q + n * P
+            nc.vector.tensor_tensor(
+                out=hi[g][q][:, n * P : (n + 1) * P, :].rearrange("p (c i) t -> p c t i", i=4),
+                in0=gps[(g, q, n)][:].rearrange("p t (c i) -> p c t i", i=4),
+                in1=vy[g][q // 2][:, :, j0 : j0 + P].rearrange("p t (c i) -> p c t i", i=4),
+                op=ADD,
+            )
+
+        def quant_h_part(g, n):
+            w = slice(n * P, (n + 1) * P)
+            nc.vector.quantize_mx(
+                out=hc[g][3][:, w].bitcast(FP8X4),
+                scales=hk[g][3][:, w],
+                in_=hi[g][3][:, w, :].rearrange("p j t -> p (j t)"),
+            )
+
+        def second_part(n, r):
+            ps = psum.tile([P, 4, P], F32, name="work_ps", tag="work")
+            cols = slice(n * P, (n + 1) * P)
+            for i in range(4):
+                w = slice((i % 2) * P, (i % 2 + 1) * P)
+                x_at = 2 * r + i // 2
+                for g in range(G):
+                    nc.tensor.matmul_mx(
+                        out=ps[:, i, :],
+                        lhsT=xc[g][x_at][:, w].bitcast(FP8X4),
+                        lhsT_scale=xk[g][x_at][:, w],
+                        rhs=hc[g][3][:, cols].bitcast(FP8X4),
+                        rhs_scale=hk[g][3][:, cols],
+                        start=(g == 0),
+                        stop=(g == G - 1),
+                    )
+            ops[("part", n, r)] = ps
+
+        def finish_part(n, r, e):
+            eng = {"V": cv, "S": cs}[e]
+            dst = os_[3][2 * n + r]
+            eng(out=dst[:].rearrange("p a b -> p (a b)"), in_=ops[("part", n, r)][:].rearrange("p a b -> p (a b)"))
+            j0 = 3 * Q + n * P
+            nc.sync.dma_start(
+                out=out[4 * r * P : 4 * (r + 1) * P, j0 : j0 + P].rearrange("(i p) j -> p i j", p=P),
+                in_=dst[:].rearrange("p a b -> p (a b)").rearrange("p (i j) -> p i j", i=4),
+            )
+
+        def quant_h(g, q):
+            nc.vector.quantize_mx(
+                out=hc[g][q][:].bitcast(FP8X4), scales=hk[g][q][:], in_=hi[g][q][:].rearrange("p j t -> p (j t)")
+            )
+
+        ops = {}
+
+        def second(q, r):
+            ps = psum.tile([P, 2, Q], F32, name="work_ps", tag="work")
+            for i in range(2):
+                w = slice(i * P, (i + 1) * P)
+                for g in range(G):
+                    nc.tensor.matmul_mx(
+                        out=ps[:, i, :],
+                        lhsT=xc[g][r][:, w].bitcast(FP8X4),
+                        lhsT_scale=xk[g][r][:, w],
+                        rhs=hc[g][q][:].bitcast(FP8X4),
+                        rhs_scale=hk[g][q][:],
+                        start=(g == 0),
+                        stop=(g == G - 1),
+                    )
+            ops[(q, r)] = ps
+
+        def finish(q, r, e):
+            eng = {"V": cv, "S": cs}[e]
+            eng(out=os_[q][r][:], in_=ops[(q, r)][:])
+            nc.sync.dma_start(
+                out=out[2 * r * P : 2 * (r + 1) * P, q * Q : (q + 1) * Q].rearrange("(i p) j -> p i j", p=P),
+                in_=os_[q][r][:],
+            )
+
+
+        keep_warm(8)
+        widen(0, 0, 3, "V")
+        widen(0, 1, 0, "S")
+        widen(0, 0, 2, "V")
+        widen(0, 0, 0, "S")
+        widen(0, 0, 1, "V")
+        widen(0, 1, 2, "V")
+        widen(0, 1, 3, "S")
+        widen(0, 1, 1, "V")
+        widen(1, 0, 1, "V")
+        widen(1, 1, 3, "S")
+        lay(0, 1, "V")
+        widen(1, 1, 0, "S")
+        widen(1, 0, 0, "S")
+        lay(0, 0, "V")
+        widen(1, 0, 2, "S")
+        turn(1, 3)
+        widen(1, 1, 1, "S")
+        widen(1, 0, 3, "V")
+        widen(1, 1, 2, "S")
+        turn(1, 2)
+        quant_x(0, 1)
+        turn_out(1, 3, "S")
+        lay(1, 1, "V")
+        turn(0, 2)
+        turn_out(1, 2, "S")
+        lay(1, 0, "V")
+        turn(0, 3)
+        keep_warm(2)
+        turn_out(0, 2, "S")
+        turn(0, 0)
+        quant_x(0, 0)
+        turn_out(0, 3, "S")
+        quant_f(1, 1)
+        turn(0, 1)
+        turn_out(0, 0, "S")
+        quant_f(0, 1)
+        turn(1, 1)
+        turn_out(0, 1, "S")
+        quant_x(1, 0)
+        turn(1, 0)
+        keep_warm(2)
+        quant_x(1, 1)
+        turn_out(1, 1, "S")
+        quant_f(0, 0)
+        turn_out(1, 0, "S")
+        nc.vector.tensor_copy(out=vf[:], in_=vb[:])
+        shift(0, 0, 1, "V")
+        first(0, 0, 1)
+        shift(0, 0, 2, "V")
+        shift(0, 0, 3, "S")
+        quant_f(1, 0)
+        first(0, 0, 0)
+        shift(0, 0, 0, "S")
+        shift(1, 0, 3, "V")
+        first(1, 0, 0)
+        shift(1, 0, 2, "S")
+        shift(1, 0, 1, "V")
+        shifted(0, 0, 1)
+        widen(1, 3, 0, "S")
+        first(1, 0, 1)
+        shift(1, 0, 0, "S")
+        shifted(0, 0, 0)
+        first(1, 1, 0)
+        widen(0, 3, 3, "S")
+        widen(1, 2, 2, "V")
+        shifted(1, 0, 0)
+        widen(0, 2, 2, "S")
+        first(0, 1, 0)
+        widen(0, 3, 0, "S")
+        shifted(1, 0, 1)
+        widen(0, 2, 1, "S")
+        first(1, 1, 1)
+        widen(0, 2, 0, "S")
+        quant_h(0, 0)
+        widen(0, 2, 3, "S")
+        quant_h(1, 0)
+        widen(1, 2, 3, "S")
+        lay(0, 2, "V")
+        second(0, 1)
+        widen(1, 3, 1, "S")
+        widen(1, 2, 0, "S")
+        shifted(0, 1, 0)
+        second(0, 0)
+        widen(1, 2, 1, "S")
+        finish(0, 1, "S")
+        first(0, 1, 1)
+        lay(1, 2, "V")
+        finish(0, 0, "S")
+        quant_x(0, 2)
+        widen(0, 3, 2, "S")
+        quant_x(1, 2)
+        widen(1, 3, 3, "S")
+        shifted(1, 1, 0)
+        second(0, 2)
+        widen(1, 3, 2, "S")
+        shift(1, 1, 2, "S")
+        shifted(0, 1, 1)
+        first(1, 2, 1)
+        lay(1, 3, "S")
+        shifted(1, 1, 1)
+        first(1, 2, 0)
+        quant_h(0, 1)
+        first(0, 2, 1)
+        quant_h(1, 1)
+        shift(1, 1, 0, "V")
+        shift(1, 1, 3, "S")
+        second(1, 0)
+        widen(0, 3, 1, "V")
+        quant_x(1, 3)
+        shift(1, 1, 1, "S")
+        second(1, 2)
+        lay(0, 3, "V")
+        finish(0, 2, "S")
+        second(1, 1)
+        shifted(1, 2, 1)
+        finish(1, 0, "S")
+        first(0, 2, 0)
+        quant_x(0, 3)
+        shift(0, 1, 3, "S")
+        shift(0, 1, 2, "V")
+        second(0, 3)
+        shift(0, 1, 0, "V")
+        shift(0, 1, 1, "S")
+        shifted(1, 2, 0)
+        second(1, 3)
+        finish(1, 2, "S")
+        shifted(0, 2, 1)
+        first(0, 3, 0)
+        finish(1, 1, "S")
+        shifted(0, 2, 0)
+        first(1, 3, 1)
+        finish(0, 3, "S")
+        quant_h(1, 2)
+        first(1, 3, 0)
+        quant_h(0, 2)
+        finish(1, 3, "S")
+        shifted(1, 3, 1)
+        second(2, 1)
+        shifted(1, 3, 0)
+        second(2, 3)
+        finish(2, 1, "S")
+        shifted(0, 3, 0)
+        second(2, 0)
+        finish(2, 3, "S")
+        quant_h_part(1, 0)
+        second(2, 2)
+        quant_h_part(0, 0)
+        quant_h_part(1, 1)
+        finish(2, 0, "S")
+        first(0, 3, 1)
+        finish(2, 2, "S")
+        second_part(0, 1)
+        shifted(0, 3, 1)
+        second_part(0, 0)
+        finish_part(0, 1, "S")
+        quant_h_part(0, 1)
+        second_part(1, 1)
+        finish_part(0, 0, "S")
+        second_part(1, 0)
+        finish_part(1, 1, "S")
+        finish_part(1, 0, "S")

@@ -45,7 +45,6 @@ def tile_loewdin_fock_shift_s7_kernel(tc, f, x_bytes, x_scale, y, v, out):
         vf = keep.tile([P, G * T], F32, name="vf")
         ident = keep.tile([P, P], F32, name="ident")
         warm = keep.tile([P, 2], F32, name="warm")
-        dz = keep.tile([P, H], BF16, name="dz", align_bytes=64)
         xb = grid("xb", G, 2, [P, T, H], U8)
         xw = grid("xw", G, 4, [P, T, Q], BF16)
         xi = grid("xi", G, 4, [P, Q, T], BF16)
@@ -77,7 +76,6 @@ def tile_loewdin_fock_shift_s7_kernel(tc, f, x_bytes, x_scale, y, v, out):
         nc.sync.dma_start(out=ys[0][1][:], in_=y_rows[0][:, :, 1*H:1*H+H])
         nc.sync.dma_start(out=ys[1][1][:], in_=y_rows[1][:, :, 1*H:1*H+H])
 
-        nc.vector.memset(dz[:], 0.0)
         nc.vector.memset(warm[:], 0.0)
         nc.scalar.activation(out=warm[:, 1:2], in_=warm[:, 0:1], func=COPY)
         make_identity(nc, ident[:])
@@ -139,12 +137,6 @@ def tile_loewdin_fock_shift_s7_kernel(tc, f, x_bytes, x_scale, y, v, out):
                 nc.vector.tensor_scalar(out=dst, in0=src, scalar1=col, scalar2=None, op0=MULT)
             else:
                 nc.gpsimd.tensor_scalar(out=dst, in0=src, scalar1=col, scalar2=0.0, op0=MULT, op1=ADD)
-
-        spin = psum.tile([P, H], F32, name="spin_ps", tag="half")
-
-        def keep_warm(count):
-            for k in range(count):
-                nc.tensor.matmul(spin[:], lhsT=dz[:, 0:P], rhs=dz[:], start=True, stop=True)
 
         gps = {}
 
@@ -242,7 +234,6 @@ def tile_loewdin_fock_shift_s7_kernel(tc, f, x_bytes, x_scale, y, v, out):
             )
 
 
-        keep_warm(8)
         widen(0, 0, 3, "V")
         widen(0, 1, 0, "S")
         widen(0, 0, 2, "V")
@@ -270,7 +261,6 @@ def tile_loewdin_fock_shift_s7_kernel(tc, f, x_bytes, x_scale, y, v, out):
         turn_out(1, 2, "S")
         lay(1, 0, "V")
         turn(0, 3)
-        keep_warm(2)
         turn_out(0, 2, "S")
         turn(0, 0)
         quant_x(0, 0)
@@ -283,7 +273,6 @@ def tile_loewdin_fock_shift_s7_kernel(tc, f, x_bytes, x_scale, y, v, out):
         turn_out(0, 1, "S")
         quant_x(1, 0)
         turn(1, 0)
-        keep_warm(2)
         quant_x(1, 1)
         turn_out(1, 1, "S")
         quant_f(0, 0)

@@ -19,8 +19,9 @@ ADD = mybir.AluOpType.add
 P = 128
 G = 2
 T = 4
-Q = 256
 H = 512
+Q = 256
+BANKS = 4
 
 
 def tile_loewdin_fock_shift_s7_kernel(tc, f, x_bytes, x_scale, y, v, out):
@@ -31,7 +32,7 @@ def tile_loewdin_fock_shift_s7_kernel(tc, f, x_bytes, x_scale, y, v, out):
 
     with ExitStack() as ctx:
         keep = ctx.enter_context(tc.tile_pool(name="keep", bufs=1))
-        psum = ctx.enter_context(tc.psum_pool(name="psum", bufs=4))
+        psum = ctx.enter_context(tc.psum_pool(name="psum", bufs=1))
         ctx.enter_context(tc.manual_schedule())
 
         def grid(name, rows, cols, shape, dtype):
@@ -40,356 +41,308 @@ def tile_loewdin_fock_shift_s7_kernel(tc, f, x_bytes, x_scale, y, v, out):
                 for a in range(rows)
             ]
 
+        def row(name, count, shape, dtype):
+            return [keep.tile(shape, dtype, name="%s_%d" % (name, a), align_bytes=64) for a in range(count)]
+
+        taken = ([], [])
+
+        def bank(ring, shape):
+            tag = "bank_%d_%d" % (ring, len(taken[ring]) % BANKS)
+            taken[ring].append(tag)
+            return psum.tile(shape, F32, name=tag, tag=tag)
+
         xs = keep.tile([P, G * T], F32, name="xs")
         vb = keep.tile([P, G * T], BF16, name="vb")
         vf = keep.tile([P, G * T], F32, name="vf")
         ident = keep.tile([P, P], F32, name="ident")
         warm = keep.tile([P, 2], F32, name="warm")
         xb = grid("xb", G, 2, [P, T, H], U8)
-        xw = grid("xw", G, 4, [P, T, Q], BF16)
-        xi = grid("xi", G, 4, [P, Q, T], BF16)
-        xc = grid("xc", G, 4, [P, Q], U32)
-        xk = grid("xk", G, 4, [P, Q], U8)
-        fs = grid("fs", G, 2, [P, 2, N], BF16)
+        left_w = row("left_w", G, [P, T, H], BF16)
+        left_i = row("left_i", G, [P, H, T], BF16)
+        left_c = row("left_c", G, [P, H], U32)
+        left_k = row("left_k", G, [P, H], U8)
+        right_w = row("right_w", 2, [P, G, T, Q], BF16)
+        right_i = row("right_i", 2, [P, G, Q, T], BF16)
+        right_c = row("right_c", 2, [P, G, Q], U32)
+        right_k = row("right_k", 2, [P, G, Q], U8)
+        fs = grid("fs", G, T, [P, N], BF16)
         fi = grid("fi", G, 2, [P, 2, G * P * T], BF16)
         fc = grid("fc", G, 2, [P, 2 * G * P], U32)
         fk = grid("fk", G, 2, [P, 2 * G * P], U8)
         ys = grid("ys", G, 2, [P, T, H], BF16)
-        vy = grid("vy", G, 2, [P, T, H], F32)
-        hi = grid("hi", G, 4, [P, Q, T], BF16)
-        hc = grid("hc", G, 4, [P, Q], U32)
-        hk = grid("hk", G, 4, [P, Q], U8)
-        os_ = grid("os", 4, 4, [P, 2, Q], F32)
+        vy = grid("vy", G, 4, [P, T, Q], F32)
+        hi = row("hi", 4, [P, G, Q, T], BF16)
+        hc = row("hc", 4, [P, G, Q], U32)
+        hk = row("hk", 4, [P, G, Q], U8)
 
-        nc.scalar.dma_start(out=xs[:], in_=x_scale.rearrange("(g p t) o -> p g (t o)", p=P, t=T))
-        nc.scalar.dma_start(out=vb[:], in_=v.rearrange("(g p t) -> p g t", p=P, t=T))
-        nc.sync.dma_start(out=xb[0][0][:], in_=x_rows[0][:, :, 0*H:0*H+H])
-        nc.sync.dma_start(out=xb[1][0][:], in_=x_rows[1][:, :, 0*H:0*H+H])
-        nc.sync.dma_start(out=fs[1][1][:], in_=f_rows[1][:, 2:4, :])
-        nc.sync.dma_start(out=fs[0][1][:], in_=f_rows[0][:, 2:4, :])
-        nc.sync.dma_start(out=fs[0][0][:], in_=f_rows[0][:, 0:2, :])
-        nc.sync.dma_start(out=fs[1][0][:], in_=f_rows[1][:, 0:2, :])
-        nc.sync.dma_start(out=ys[0][0][:], in_=y_rows[0][:, :, 0*H:0*H+H])
-        nc.sync.dma_start(out=ys[1][0][:], in_=y_rows[1][:, :, 0*H:0*H+H])
-        nc.sync.dma_start(out=xb[1][1][:], in_=x_rows[1][:, :, 1*H:1*H+H])
-        nc.sync.dma_start(out=xb[0][1][:], in_=x_rows[0][:, :, 1*H:1*H+H])
-        nc.sync.dma_start(out=ys[0][1][:], in_=y_rows[0][:, :, 1*H:1*H+H])
-        nc.sync.dma_start(out=ys[1][1][:], in_=y_rows[1][:, :, 1*H:1*H+H])
+        copy = {"V": nc.vector.tensor_copy, "S": nc.scalar.copy}
 
-        nc.vector.memset(warm[:], 0.0)
-        nc.scalar.activation(out=warm[:, 1:2], in_=warm[:, 0:1], func=COPY)
-        make_identity(nc, ident[:])
+        def load_x(g, h):
+            nc.sync.dma_start(out=xb[g][h][:], in_=x_rows[g][:, :, h * H : (h + 1) * H])
 
-        cv = nc.vector.tensor_copy
-        cs = nc.scalar.copy
+        def load_f(g, t):
+            nc.sync.dma_start(out=fs[g][t][:], in_=f_rows[g][:, t, :])
 
-        def widen(g, q, t, eng):
-            (widen_v if eng == "V" else widen_s)(g, q, t)
+        def load_y(g, h):
+            nc.sync.dma_start(out=ys[g][h][:], in_=y_rows[g][:, :, h * H : (h + 1) * H])
 
-        def widen_s(g, q, t):
-            src = xb[g][q // 2][:, t, (q % 2) * Q : (q % 2 + 1) * Q].bitcast(FP8)
-            nc.scalar.activation(out=xw[g][q][:, t, :], in_=src, func=COPY, scale=xs[:, g * T + t : g * T + t + 1])
+        def times_column(dst, src, column, eng):
+            if eng == "V":
+                nc.vector.tensor_scalar(out=dst, in0=src, scalar1=column, scalar2=None, op0=MULT)
+            else:
+                nc.scalar.activation(out=dst, in_=src, func=COPY, scale=column)
 
-        def widen_v(g, q, t):
-            src = xb[g][q // 2][:, t, (q % 2) * Q : (q % 2 + 1) * Q].bitcast(FP8)
-            nc.vector.tensor_scalar(
-                out=xw[g][q][:, t, :], in0=src, scalar1=xs[:, g * T + t : g * T + t + 1], scalar2=None, op0=MULT
+        def widen_left(g, t, eng):
+            times_column(left_w[g][:, t, :], xb[g][0][:, t, :].bitcast(FP8), xs[:, g * T + t : g * T + t + 1], eng)
+
+        def widen_right(q, g, t, eng):
+            src = xb[g][1][:, t, (q - 2) * Q : (q - 1) * Q].bitcast(FP8)
+            times_column(right_w[q - 2][:, g, t, :], src, xs[:, g * T + t : g * T + t + 1], eng)
+
+        def quant(mixed, codes, scales):
+            nc.vector.quantize_mx(out=codes.bitcast(FP8X4), scales=scales, in_=mixed)
+
+        def lay_left(g):
+            nc.vector.tensor_copy(
+                out=left_i[g][:].rearrange("p (c i) t -> p c t i", i=4),
+                in_=left_w[g][:].rearrange("p t (c i) -> p c t i", i=4),
             )
 
-        def lay(g, q, eng):
-            (nc.vector.tensor_copy if eng == "V" else nc.scalar.copy)(
-                out=xi[g][q][:].rearrange("p (c i) t -> p c t i", i=4),
-                in_=xw[g][q][:].rearrange("p t (c i) -> p c t i", i=4),
+        def lay_right(q):
+            nc.vector.tensor_copy(
+                out=right_i[q - 2][:].rearrange("p g (c i) t -> p g c t i", i=4),
+                in_=right_w[q - 2][:].rearrange("p g t (c i) -> p g c t i", i=4),
             )
 
-        def quant_x(g, q):
-            nc.vector.quantize_mx(
-                out=xc[g][q][:].bitcast(FP8X4), scales=xk[g][q][:], in_=xi[g][q][:].rearrange("p j t -> p (j t)")
+        def quant_left(g):
+            quant(left_i[g][:].rearrange("p j t -> p (j t)"), left_c[g][:], left_k[g][:])
+
+        def quant_right(q):
+            quant(
+                right_i[q - 2][:].rearrange("p g j t -> p (g j t)"),
+                right_c[q - 2][:].rearrange("p g j -> p (g j)"),
+                right_k[q - 2][:].rearrange("p g j -> p (g j)"),
             )
 
-        tps = {}
+        def x_operand(g, j0):
+            if j0 < H:
+                return left_c[g][:, j0 : j0 + P].bitcast(FP8X4), left_k[g][:, j0 : j0 + P]
+            q, lo = divmod(j0 - H, Q)
+            return right_c[q][:, g, lo : lo + P].bitcast(FP8X4), right_k[q][:, g, lo : lo + P]
+
+        def quant_h(q):
+            quant(
+                hi[q][:].rearrange("p g j t -> p (g j t)"),
+                hc[q][:].rearrange("p g j -> p (g j)"),
+                hk[q][:].rearrange("p g j -> p (g j)"),
+            )
+
+        turned = {}
 
         def turn(g, t):
-            ps = psum.tile([P, G, 2, P], F32, name="work_ps", tag="work")
-            words = fs[g][t // 2][:, t % 2, :].bitcast(F32)
+            ps = bank(g, [P, G, 2, P])
+            words = fs[g][t][:].bitcast(F32)
             for c in range(G):
                 for u in range(2):
                     nc.tensor.transpose(ps[:, c, u, :], words[:, 256 * c + u : 256 * (c + 1) : 2], ident[:])
-            tps[(g, t)] = ps
+            turned[(g, t)] = ps
 
-        def turn_out(g, t, e):
-            eng = {"V": cv, "S": cs}[e]
+        def turn_out(g, t, eng):
             dst = fi[g][t // 2][:, t % 2, :].bitcast(F32).rearrange("p (c r u) -> p c r u", c=G, u=2)
-            eng(out=dst, in_=tps[(g, t)][:].rearrange("p c u r -> p c r u"))
+            copy[eng](out=dst, in_=turned[(g, t)][:].rearrange("p c u r -> p c r u"))
 
         def quant_f(g, r):
             nc.vector.quantize_mx(
                 out=fc[g][r][:].bitcast(FP8X4), scales=fk[g][r][:], in_=fi[g][r][:].rearrange("p s k -> p (s k)")
             )
 
-        def shift(g, h, t, eng):
-            src = ys[g][h][:, t, :]
-            dst = vy[g][h][:, t, :]
-            col = vf[:, g * T + t : g * T + t + 1]
-            if eng == "S":
-                nc.scalar.activation(out=dst, in_=src, func=COPY, scale=col)
-            elif eng == "V":
-                nc.vector.tensor_scalar(out=dst, in0=src, scalar1=col, scalar2=None, op0=MULT)
-            else:
-                nc.gpsimd.tensor_scalar(out=dst, in0=src, scalar1=col, scalar2=0.0, op0=MULT, op1=ADD)
+        def scale_y(q, g, engines):
+            for t, eng in enumerate(engines):
+                if eng != "-":
+                    src = ys[g][q // 2][:, t, (q % 2) * Q : (q % 2 + 1) * Q]
+                    times_column(vy[g][q][:, t, :], src, vf[:, g * T + t : g * T + t + 1], eng)
 
-        gps = {}
+        half_done = {}
 
-        def first(g, q, n):
-            ps = psum.tile([P, T, P], F32, name="half_ps", tag="half")
-            cols = slice(n * P, (n + 1) * P)
+        def first(q, g, n, ring):
+            ps = bank(ring, [P, T, P])
             for t in range(T):
                 for c in range(G):
-                    w = slice((t % 2) * 2 * P + c * P, (t % 2) * 2 * P + (c + 1) * P)
+                    w = slice(((t % 2) * G + c) * P, ((t % 2) * G + c + 1) * P)
+                    codes, scales = x_operand(c, q * Q + n * P)
                     nc.tensor.matmul_mx(
                         out=ps[:, t, :],
                         lhsT=fc[g][t // 2][:, w].bitcast(FP8X4),
                         lhsT_scale=fk[g][t // 2][:, w],
-                        rhs=xc[c][q][:, cols].bitcast(FP8X4),
-                        rhs_scale=xk[c][q][:, cols],
+                        rhs=codes,
+                        rhs_scale=scales,
                         start=(c == 0),
                         stop=(c == G - 1),
                     )
-            gps[(g, q, n)] = ps
+            half_done[(q, g, n)] = ps
 
-        def shifted(g, q, n):
-            j0 = (q % 2) * Q + n * P
+        def h_slot(tile, q, g, n):
+            a, b = (n, g) if q == 3 else (g, n)
+            return tile[q][:, a, b * P : (b + 1) * P]
+
+        def shift(q, g, n):
+            addend = vy[g][q][:, :, n * P : (n + 1) * P]
             nc.vector.tensor_tensor(
-                out=hi[g][q][:, n * P : (n + 1) * P, :].rearrange("p (c i) t -> p c t i", i=4),
-                in0=gps[(g, q, n)][:].rearrange("p t (c i) -> p c t i", i=4),
-                in1=vy[g][q // 2][:, :, j0 : j0 + P].rearrange("p t (c i) -> p c t i", i=4),
+                out=h_slot(hi, q, g, n).rearrange("p (c i) t -> p c t i", i=4),
+                in0=half_done[(q, g, n)][:].rearrange("p t (c i) -> p c t i", i=4),
+                in1=addend.rearrange("p t (c i) -> p c t i", i=4),
                 op=ADD,
             )
 
-        def quant_h_part(g, n):
-            w = slice(n * P, (n + 1) * P)
-            nc.vector.quantize_mx(
-                out=hc[g][3][:, w].bitcast(FP8X4),
-                scales=hk[g][3][:, w],
-                in_=hi[g][3][:, w, :].rearrange("p j t -> p (j t)"),
-            )
+        def quant_last(n):
+            quant(hi[3][:, n].rearrange("p j t -> p (j t)"), hc[3][:, n, :], hk[3][:, n, :])
 
-        def second_part(n, r):
-            ps = psum.tile([P, 4, P], F32, name="work_ps", tag="work")
-            cols = slice(n * P, (n + 1) * P)
-            for i in range(4):
-                w = slice((i % 2) * P, (i % 2 + 1) * P)
-                x_at = 2 * r + i // 2
+        sums = {}
+
+        def second(q, b, ring):
+            ps = bank(ring, [P, 2, Q])
+            for n in range(2):
                 for g in range(G):
+                    codes, scales = x_operand(g, (2 * b + n) * P)
                     nc.tensor.matmul_mx(
-                        out=ps[:, i, :],
-                        lhsT=xc[g][x_at][:, w].bitcast(FP8X4),
-                        lhsT_scale=xk[g][x_at][:, w],
-                        rhs=hc[g][3][:, cols].bitcast(FP8X4),
-                        rhs_scale=hk[g][3][:, cols],
+                        out=ps[:, n, :],
+                        lhsT=codes,
+                        lhsT_scale=scales,
+                        rhs=hc[q][:, g, :].bitcast(FP8X4),
+                        rhs_scale=hk[q][:, g, :],
                         start=(g == 0),
                         stop=(g == G - 1),
                     )
-            ops[("part", n, r)] = ps
+            sums[(q * Q, 2 * b)] = ps
 
-        def finish_part(n, r, e):
-            eng = {"V": cv, "S": cs}[e]
-            dst = os_[3][2 * n + r]
-            eng(out=dst[:].rearrange("p a b -> p (a b)"), in_=ops[("part", n, r)][:].rearrange("p a b -> p (a b)"))
-            j0 = 3 * Q + n * P
-            nc.sync.dma_start(
-                out=out[4 * r * P : 4 * (r + 1) * P, j0 : j0 + P].rearrange("(i p) j -> p i j", p=P),
-                in_=dst[:].rearrange("p a b -> p (a b)").rearrange("p (i j) -> p i j", i=4),
-            )
-
-        def quant_h(g, q):
-            nc.vector.quantize_mx(
-                out=hc[g][q][:].bitcast(FP8X4), scales=hk[g][q][:], in_=hi[g][q][:].rearrange("p j t -> p (j t)")
-            )
-
-        ops = {}
-
-        def second(q, r):
-            ps = psum.tile([P, 2, Q], F32, name="work_ps", tag="work")
-            for i in range(2):
-                w = slice(i * P, (i + 1) * P)
+        def second_last(n, i0, count, ring):
+            ps = bank(ring, [P, count, P])
+            for i in range(count):
                 for g in range(G):
+                    codes, scales = x_operand(g, (i0 + i) * P)
                     nc.tensor.matmul_mx(
                         out=ps[:, i, :],
-                        lhsT=xc[g][r][:, w].bitcast(FP8X4),
-                        lhsT_scale=xk[g][r][:, w],
-                        rhs=hc[g][q][:].bitcast(FP8X4),
-                        rhs_scale=hk[g][q][:],
+                        lhsT=codes,
+                        lhsT_scale=scales,
+                        rhs=h_slot(hc, 3, g, n).bitcast(FP8X4),
+                        rhs_scale=h_slot(hk, 3, g, n),
                         start=(g == 0),
                         stop=(g == G - 1),
                     )
-            ops[(q, r)] = ps
+            sums[(3 * Q + n * P, i0)] = ps
 
-        def finish(q, r, e):
-            eng = {"V": cv, "S": cs}[e]
-            eng(out=os_[q][r][:], in_=ops[(q, r)][:])
+        def finish(j0, i0, eng):
+            ps = sums[(j0, i0)]
+            count, width = ps.shape[1], ps.shape[2]
+            res = keep.tile([P, count, width], F32, name="res_%d_%d" % (j0, i0))
+            copy[eng](out=res[:], in_=ps[:])
             nc.sync.dma_start(
-                out=out[2 * r * P : 2 * (r + 1) * P, q * Q : (q + 1) * Q].rearrange("(i p) j -> p i j", p=P),
-                in_=os_[q][r][:],
+                out=out[i0 * P : (i0 + count) * P, j0 : j0 + width].rearrange("(i p) j -> p i j", p=P), in_=res[:]
             )
 
+        nc.scalar.dma_start(out=xs[:], in_=x_scale.rearrange("(g p t) o -> p g (t o)", p=P, t=T))
+        nc.scalar.dma_start(out=vb[:], in_=v.rearrange("(g p t) -> p g t", p=P, t=T))
+        for g in range(G):
+            load_x(g, 0)
+        for g in range(G):
+            for t in range(T):
+                load_f(g, t)
+        load_y(0, 0)
+        load_y(1, 0)
+        for g in range(G):
+            load_x(g, 1)
+        for g in range(G):
+            load_y(g, 1)
 
-        widen(0, 0, 3, "V")
-        widen(0, 1, 0, "S")
-        widen(0, 0, 2, "V")
-        widen(0, 0, 0, "S")
-        widen(0, 0, 1, "V")
-        widen(0, 1, 2, "V")
-        widen(0, 1, 3, "S")
-        widen(0, 1, 1, "V")
-        widen(1, 0, 1, "V")
-        widen(1, 1, 3, "S")
-        lay(0, 1, "V")
-        widen(1, 1, 0, "S")
-        widen(1, 0, 0, "S")
-        lay(0, 0, "V")
-        widen(1, 0, 2, "S")
-        turn(1, 3)
-        widen(1, 1, 1, "S")
-        widen(1, 0, 3, "V")
-        widen(1, 1, 2, "S")
-        turn(1, 2)
-        quant_x(0, 1)
-        turn_out(1, 3, "S")
-        lay(1, 1, "V")
-        turn(0, 2)
-        turn_out(1, 2, "S")
-        lay(1, 0, "V")
-        turn(0, 3)
-        turn_out(0, 2, "S")
-        turn(0, 0)
-        quant_x(0, 0)
-        turn_out(0, 3, "S")
-        quant_f(1, 1)
-        turn(0, 1)
-        turn_out(0, 0, "S")
-        quant_f(0, 1)
-        turn(1, 1)
-        turn_out(0, 1, "S")
-        quant_x(1, 0)
-        turn(1, 0)
-        quant_x(1, 1)
-        turn_out(1, 1, "S")
+        nc.vector.memset(warm[:], 0.0)
+        nc.scalar.activation(out=warm[:, 1:2], in_=warm[:, 0:1], func=COPY)
+        make_identity(nc, ident[:])
+
+        for t, eng in enumerate("VSVV"):
+            widen_left(0, t, eng)
+        lay_left(0)
+        for t, eng in enumerate("SSSV"):
+            widen_left(1, t, eng)
+        quant_left(0)
+        lay_left(1)
+        for g in range(G):
+            for t in range(T):
+                turn(g, t)
+                turn_out(g, t, "S")
         quant_f(0, 0)
-        turn_out(1, 0, "S")
+        quant_left(1)
+        quant_f(0, 1)
         nc.vector.tensor_copy(out=vf[:], in_=vb[:])
-        shift(0, 0, 1, "V")
-        first(0, 0, 1)
-        shift(0, 0, 2, "V")
-        shift(0, 0, 3, "S")
         quant_f(1, 0)
-        first(0, 0, 0)
-        shift(0, 0, 0, "S")
-        shift(1, 0, 3, "V")
-        first(1, 0, 0)
-        shift(1, 0, 2, "S")
-        shift(1, 0, 1, "V")
-        shifted(0, 0, 1)
-        widen(1, 3, 0, "S")
-        first(1, 0, 1)
-        shift(1, 0, 0, "S")
-        shifted(0, 0, 0)
-        first(1, 1, 0)
-        widen(0, 3, 3, "S")
-        widen(1, 2, 2, "V")
-        shifted(1, 0, 0)
-        widen(0, 2, 2, "S")
-        first(0, 1, 0)
-        widen(0, 3, 0, "S")
-        shifted(1, 0, 1)
-        widen(0, 2, 1, "S")
-        first(1, 1, 1)
-        widen(0, 2, 0, "S")
-        quant_h(0, 0)
-        widen(0, 2, 3, "S")
-        quant_h(1, 0)
-        widen(1, 2, 3, "S")
-        lay(0, 2, "V")
-        second(0, 1)
-        widen(1, 3, 1, "S")
-        widen(1, 2, 0, "S")
-        shifted(0, 1, 0)
-        second(0, 0)
-        widen(1, 2, 1, "S")
-        finish(0, 1, "S")
-        first(0, 1, 1)
-        lay(1, 2, "V")
-        finish(0, 0, "S")
-        quant_x(0, 2)
-        widen(0, 3, 2, "S")
-        quant_x(1, 2)
-        widen(1, 3, 3, "S")
-        shifted(1, 1, 0)
-        second(0, 2)
-        widen(1, 3, 2, "S")
-        shift(1, 1, 2, "S")
-        shifted(0, 1, 1)
-        first(1, 2, 1)
-        lay(1, 3, "S")
-        shifted(1, 1, 1)
-        first(1, 2, 0)
-        quant_h(0, 1)
-        first(0, 2, 1)
-        quant_h(1, 1)
-        shift(1, 1, 0, "V")
-        shift(1, 1, 3, "S")
-        second(1, 0)
-        widen(0, 3, 1, "V")
-        quant_x(1, 3)
-        shift(1, 1, 1, "S")
-        second(1, 2)
-        lay(0, 3, "V")
-        finish(0, 2, "S")
-        second(1, 1)
-        shifted(1, 2, 1)
-        finish(1, 0, "S")
-        first(0, 2, 0)
-        quant_x(0, 3)
-        shift(0, 1, 3, "S")
-        shift(0, 1, 2, "V")
-        second(0, 3)
-        shift(0, 1, 0, "V")
-        shift(0, 1, 1, "S")
-        shifted(1, 2, 0)
-        second(1, 3)
-        finish(1, 2, "S")
-        shifted(0, 2, 1)
-        first(0, 3, 0)
-        finish(1, 1, "S")
-        shifted(0, 2, 0)
-        first(1, 3, 1)
-        finish(0, 3, "S")
-        quant_h(1, 2)
-        first(1, 3, 0)
-        quant_h(0, 2)
-        finish(1, 3, "S")
-        shifted(1, 3, 1)
-        second(2, 1)
-        shifted(1, 3, 0)
-        second(2, 3)
-        finish(2, 1, "S")
-        shifted(0, 3, 0)
-        second(2, 0)
-        finish(2, 3, "S")
-        quant_h_part(1, 0)
-        second(2, 2)
-        quant_h_part(0, 0)
-        quant_h_part(1, 1)
-        finish(2, 0, "S")
-        first(0, 3, 1)
-        finish(2, 2, "S")
-        second_part(0, 1)
-        shifted(0, 3, 1)
-        second_part(0, 0)
-        finish_part(0, 1, "S")
-        quant_h_part(0, 1)
-        second_part(1, 1)
-        finish_part(0, 0, "S")
-        second_part(1, 0)
-        finish_part(1, 1, "S")
-        finish_part(1, 0, "S")
+        scale_y(0, 0, "VVSS")
+        quant_f(1, 1)
+        scale_y(0, 1, "VVSS")
+        for q in range(2):
+            for g in range(G):
+                for n in range(2):
+                    first(q, g, n, q)
+        for g in range(G):
+            for t in range(T):
+                widen_right(2, g, t, "S")
+        for g in range(G):
+            for n in range(2):
+                shift(0, g, n)
+        scale_y(1, 0, "VSSS")
+        quant_h(0)
+        scale_y(1, 1, "SSSS")
+        lay_right(2)
+        for b in range(2):
+            second(0, b, 0)
+        shift(1, 0, 0)
+        quant_right(2)
+        for b in range(2):
+            finish(0, 2 * b, "S")
+        for g in range(G):
+            for t in range(T):
+                widen_right(3, g, t, "S")
+        shift(1, 0, 1)
+        for n in range(2):
+            first(2, 0, n, 0)
+        for n in range(2):
+            shift(1, 1, n)
+        second(0, 2, 1)
+        for n in range(2):
+            first(2, 1, n, 0)
+        finish(0, 4, "S")
+        scale_y(2, 0, "VV--")
+        quant_h(1)
+        lay_right(3)
+        scale_y(2, 0, "--VV")
+        quant_right(3)
+        scale_y(2, 1, "SSSS")
+        for b in range(3):
+            second(1, b, 1)
+            finish(Q, 2 * b, "S")
+        for q in range(2):
+            second(q, 3, 1)
+            finish(q * Q, 6, "S")
+        for g in range(G):
+            for n in range(2):
+                shift(2, g, n)
+        for n in range(2):
+            for g in range(G):
+                first(3, g, n, 0)
+        scale_y(3, 0, "V-SS")
+        quant_h(2)
+        scale_y(3, 0, "-V--")
+        scale_y(3, 1, "VSSS")
+        for b in range(4):
+            second(2, b, 1)
+            finish(2 * Q, 2 * b, "S")
+        shift(3, 0, 0)
+        shift(3, 1, 0)
+        shift(3, 0, 1)
+        quant_last(0)
+        shift(3, 1, 1)
+        quant_last(1)
+        for i0 in (0, 4):
+            second_last(0, i0, 4, 0)
+            finish(3 * Q, i0, "S")
+        for i0 in range(0, 8, 2):
+            second_last(1, i0, 2, 1 - i0 // 4)
+            finish(3 * Q + P, i0, "VS"[i0 // 2 % 2])

@@ -336,13 +336,13 @@ def tile_loewdin_fock_shift_s7_kernel(tc, f, x_bytes, x_scale, y, v, out):
             finish(2 * Q, 2 * b, "S")
         shift(3, 0, 0)
         shift(3, 1, 0)
-        shift(3, 0, 1)
         quant_last(0)
+        shift(3, 0, 1)
         shift(3, 1, 1)
         quant_last(1)
-        for i0 in (0, 4):
-            second_last(0, i0, 4, 0)
-            finish(3 * Q, i0, "S")
         for i0 in range(0, 8, 2):
-            second_last(1, i0, 2, 1 - i0 // 4)
-            finish(3 * Q + P, i0, "VS"[i0 // 2 % 2])
+            second_last(0, i0, 2, 0)
+            finish(3 * Q, i0, "SSSV"[i0 // 2])
+        for i0 in range(0, 8, 2):
+            second_last(1, i0, 2, 1)
+            finish(3 * Q + P, i0, "SV"[i0 // 2 % 2])

@@ -37,12 +37,12 @@ def tile_loewdin_fock_shift_s7_kernel(tc, f, x_bytes, x_scale, y, v, out):
 
         def grid(name, rows, cols, shape, dtype):
             return [
-                [keep.tile(shape, dtype, name="%s_%d_%d" % (name, a, b), align_bytes=64) for b in range(cols)]
+                [keep.tile(shape, dtype, name="%s_%d_%d" % (name, a, b), align_bytes=256) for b in range(cols)]
                 for a in range(rows)
             ]
 
         def row(name, count, shape, dtype):
-            return [keep.tile(shape, dtype, name="%s_%d" % (name, a), align_bytes=64) for a in range(count)]
+            return [keep.tile(shape, dtype, name="%s_%d" % (name, a), align_bytes=256) for a in range(count)]
 
         taken = ([], [])
 
@@ -234,7 +234,7 @@ def tile_loewdin_fock_shift_s7_kernel(tc, f, x_bytes, x_scale, y, v, out):
         def finish(j0, i0, eng):
             ps = sums[(j0, i0)]
             count, width = ps.shape[1], ps.shape[2]
-            res = keep.tile([P, count, width], F32, name="res_%d_%d" % (j0, i0))
+            res = keep.tile([P, count, width], F32, name="res_%d_%d" % (j0, i0), align_bytes=256)
             copy[eng](out=res[:], in_=ps[:])
             nc.sync.dma_start(
                 out=out[i0 * P : (i0 + count) * P, j0 : j0 + width].rearrange("(i p) j -> p i j", p=P), in_=res[:]

@@ -51,12 +51,13 @@ def tile_loewdin_fock_shift_s7_kernel(tc, f, x_bytes, x_scale, y, v, out):
             taken[ring].append(tag)
             return psum.tile(shape, F32, name=tag, tag=tag)
 
-        xs = keep.tile([P, G * T], F32, name="xs")
+        xs = [keep.tile([P, T], F32, name="xs_%d" % g) for g in range(G)]
         vb = keep.tile([P, G * T], BF16, name="vb")
         vf = keep.tile([P, G * T], F32, name="vf")
         ident = keep.tile([P, P], F32, name="ident")
         warm = keep.tile([P, 2], F32, name="warm")
-        xb = grid("xb", G, 2, [P, T, H], U8)
+        left_b = grid("left_b", G, 2, [P, 2, H], U8)
+        right_b = row("right_b", G, [P, T, H], U8)
         left_w = row("left_w", G, [P, T, H], BF16)
         left_i = row("left_i", G, [P, H, T], BF16)
         left_c = row("left_c", G, [P, H], U32)
@@ -69,7 +70,8 @@ def tile_loewdin_fock_shift_s7_kernel(tc, f, x_bytes, x_scale, y, v, out):
         fi = grid("fi", G, 2, [P, 2, G * P * T], BF16)
         fc = grid("fc", G, 2, [P, 2 * G * P], U32)
         fk = grid("fk", G, 2, [P, 2 * G * P], U8)
-        ys = grid("ys", G, 2, [P, T, H], BF16)
+        left_y = grid("left_y", G, 2, [P, T, Q], BF16)
+        right_y = row("right_y", G, [P, T, H], BF16)
         vy = grid("vy", G, 4, [P, T, Q], F32)
         hi = row("hi", 4, [P, G, Q, T], BF16)
         hc = row("hc", 4, [P, G, Q], U32)
@@ -77,14 +79,8 @@ def tile_loewdin_fock_shift_s7_kernel(tc, f, x_bytes, x_scale, y, v, out):
 
         copy = {"V": nc.vector.tensor_copy, "S": nc.scalar.copy}
 
-        def load_x(g, h):
-            nc.sync.dma_start(out=xb[g][h][:], in_=x_rows[g][:, :, h * H : (h + 1) * H])
-
         def load_f(g, t):
             nc.sync.dma_start(out=fs[g][t][:], in_=f_rows[g][:, t, :])
-
-        def load_y(g, h):
-            nc.sync.dma_start(out=ys[g][h][:], in_=y_rows[g][:, :, h * H : (h + 1) * H])
 
         def times_column(dst, src, column, eng):
             if eng == "V":
@@ -93,11 +89,12 @@ def tile_loewdin_fock_shift_s7_kernel(tc, f, x_bytes, x_scale, y, v, out):
                 nc.scalar.activation(out=dst, in_=src, func=COPY, scale=column)
 
         def widen_left(g, t, eng):
-            times_column(left_w[g][:, t, :], xb[g][0][:, t, :].bitcast(FP8), xs[:, g * T + t : g * T + t + 1], eng)
+            src = left_b[g][t // 2][:, t % 2, :]
+            times_column(left_w[g][:, t, :], src.bitcast(FP8), xs[g][:, t : t + 1], eng)
 
         def widen_right(q, g, t, eng):
-            src = xb[g][1][:, t, (q - 2) * Q : (q - 1) * Q].bitcast(FP8)
-            times_column(right_w[q - 2][:, g, t, :], src, xs[:, g * T + t : g * T + t + 1], eng)
+            src = right_b[g][:, t, (q - 2) * Q : (q - 1) * Q].bitcast(FP8)
+            times_column(right_w[q - 2][:, g, t, :], src, xs[g][:, t : t + 1], eng)
 
         def quant(mixed, codes, scales):
             nc.vector.quantize_mx(out=codes.bitcast(FP8X4), scales=scales, in_=mixed)
@@ -137,6 +134,9 @@ def tile_loewdin_fock_shift_s7_kernel(tc, f, x_bytes, x_scale, y, v, out):
                 hk[q][:].rearrange("p g j -> p (g j)"),
             )
 
+        def quant_h_pass(q, g):
+            quant(hi[q][:, g].rearrange("p j t -> p (j t)"), hc[q][:, g, :], hk[q][:, g, :])
+
         turned = {}
 
         def turn(g, t):
@@ -159,7 +159,7 @@ def tile_loewdin_fock_shift_s7_kernel(tc, f, x_bytes, x_scale, y, v, out):
         def scale_y(q, g, engines):
             for t, eng in enumerate(engines):
                 if eng != "-":
-                    src = ys[g][q // 2][:, t, (q % 2) * Q : (q % 2 + 1) * Q]
+                    src = left_y[g][q][:, t, :] if q < 2 else right_y[g][:, t, (q - 2) * Q : (q - 1) * Q]
                     times_column(vy[g][q][:, t, :], src, vf[:, g * T + t : g * T + t + 1], eng)
 
         half_done = {}
@@ -195,7 +195,8 @@ def tile_loewdin_fock_shift_s7_kernel(tc, f, x_bytes, x_scale, y, v, out):
             )
 
         def quant_last(n):
-            quant(hi[3][:, n].rearrange("p j t -> p (j t)"), hc[3][:, n, :], hk[3][:, n, :])
+            for g in range(G):
+                quant(h_slot(hi, 3, g, n).rearrange("p j t -> p (j t)"), h_slot(hc, 3, g, n), h_slot(hk, 3, g, n))
 
         sums = {}
 
@@ -240,19 +241,23 @@ def tile_loewdin_fock_shift_s7_kernel(tc, f, x_bytes, x_scale, y, v, out):
                 out=out[i0 * P : (i0 + count) * P, j0 : j0 + width].rearrange("(i p) j -> p i j", p=P), in_=res[:]
             )
 
-        nc.scalar.dma_start(out=xs[:], in_=x_scale.rearrange("(g p t) o -> p g (t o)", p=P, t=T))
-        nc.scalar.dma_start(out=vb[:], in_=v.rearrange("(g p t) -> p g t", p=P, t=T))
+        scale_rows = x_scale.rearrange("(g p t) o -> g p (t o)", p=P, t=T)
         for g in range(G):
-            load_x(g, 0)
+            nc.scalar.dma_start(out=xs[g][:], in_=scale_rows[g])
+        for g in range(G):
+            for r in range(2):
+                nc.sync.dma_start(out=left_b[g][r][:], in_=x_rows[g][:, 2 * r : 2 * r + 2, 0:H])
         for g in range(G):
             for t in range(T):
                 load_f(g, t)
-        load_y(0, 0)
-        load_y(1, 0)
         for g in range(G):
-            load_x(g, 1)
+            nc.sync.dma_start(out=left_y[g][0][:], in_=y_rows[g][:, :, 0:Q])
         for g in range(G):
-            load_y(g, 1)
+            nc.sync.dma_start(out=right_b[g][:], in_=x_rows[g][:, :, H:N])
+        for g in range(G):
+            nc.sync.dma_start(out=left_y[g][1][:], in_=y_rows[g][:, :, Q:H])
+        for g in range(G):
+            nc.sync.dma_start(out=right_y[g][:], in_=y_rows[g][:, :, H:N])
 
         nc.vector.memset(warm[:], 0.0)
         nc.scalar.activation(out=warm[:, 1:2], in_=warm[:, 0:1], func=COPY)
@@ -260,11 +265,12 @@ def tile_loewdin_fock_shift_s7_kernel(tc, f, x_bytes, x_scale, y, v, out):
 
         for t, eng in enumerate("VSVV"):
             widen_left(0, t, eng)
-        lay_left(0)
-        for t, eng in enumerate("SSSV"):
+        for t, eng in enumerate("VSSS"):
             widen_left(1, t, eng)
-        quant_left(0)
+        lay_left(0)
+        nc.scalar.dma_start(out=vb[:], in_=v.rearrange("(g p t) -> p g t", p=P, t=T))
         lay_left(1)
+        quant_left(0)
         for g in range(G):
             for t in range(T):
                 turn(g, t)
@@ -287,7 +293,7 @@ def tile_loewdin_fock_shift_s7_kernel(tc, f, x_bytes, x_scale, y, v, out):
         for g in range(G):
             for n in range(2):
                 shift(0, g, n)
-        scale_y(1, 0, "VSSS")
+        scale_y(1, 0, "VVSS")
         quant_h(0)
         scale_y(1, 1, "SSSS")
         lay_right(2)
@@ -308,32 +314,35 @@ def tile_loewdin_fock_shift_s7_kernel(tc, f, x_bytes, x_scale, y, v, out):
         second(0, 2, 1)
         for n in range(2):
             first(2, 1, n, 0)
+        scale_y(2, 0, "SSS-")
         finish(0, 4, "S")
-        scale_y(2, 0, "VV--")
-        quant_h(1)
+        for g in range(G):
+            quant_h_pass(1, g)
         lay_right(3)
-        scale_y(2, 0, "--VV")
+        scale_y(2, 0, "---V")
         quant_right(3)
         scale_y(2, 1, "SSSS")
         for b in range(3):
             second(1, b, 1)
             finish(Q, 2 * b, "S")
-        for q in range(2):
-            second(q, 3, 1)
-            finish(q * Q, 6, "S")
+        second(0, 3, 1)
+        finish(0, 6, "S")
         for g in range(G):
             for n in range(2):
                 shift(2, g, n)
-        for n in range(2):
-            for g in range(G):
-                first(3, g, n, 0)
-        scale_y(3, 0, "V-SS")
-        quant_h(2)
-        scale_y(3, 0, "-V--")
+        first(3, 0, 0, 0)
+        second(1, 3, 1)
+        finish(Q, 6, "S")
+        first(3, 1, 0, 0)
+        first(3, 0, 1, 0)
+        for g in range(G):
+            quant_h_pass(2, g)
+        scale_y(3, 0, "VVVV")
         scale_y(3, 1, "VSSS")
         for b in range(4):
             second(2, b, 1)
             finish(2 * Q, 2 * b, "S")
+        first(3, 1, 1, 0)
         shift(3, 0, 0)
         shift(3, 1, 0)
         quant_last(0)
@@ -341,8 +350,8 @@ def tile_loewdin_fock_shift_s7_kernel(tc, f, x_bytes, x_scale, y, v, out):
         shift(3, 1, 1)
         quant_last(1)
         for i0 in range(0, 8, 2):
-            second_last(0, i0, 2, 0)
+            second_last(0, i0, 2, i0 // 6)
             finish(3 * Q, i0, "SSSV"[i0 // 2])
         for i0 in range(0, 8, 2):
-            second_last(1, i0, 2, 1)
+            second_last(1, i0, 2, 1 - i0 // 6)
             finish(3 * Q + P, i0, "SV"[i0 // 2 % 2])

@@ -1,7 +1,6 @@
 from contextlib import ExitStack
 
 import concourse.mybir as mybir
-from concourse.masks import make_identity
 
 N = 1024
 FLOPS = 2 * 2 * N * N * N
@@ -9,10 +8,12 @@ FLOPS = 2 * 2 * N * N * N
 F32 = mybir.dt.float32
 BF16 = mybir.dt.bfloat16
 U32 = mybir.dt.uint32
+I32 = mybir.dt.int32
 U8 = mybir.dt.uint8
 FP8 = mybir.dt.float8_e4m3fn
 FP8X4 = mybir.dt.float8_e4m3fn_x4
 COPY = mybir.ActivationFunctionType.Copy
+RELU = mybir.ActivationFunctionType.Relu
 MULT = mybir.AluOpType.mult
 ADD = mybir.AluOpType.add
 
@@ -51,13 +52,12 @@ def tile_loewdin_fock_shift_s7_kernel(tc, f, x_bytes, x_scale, y, v, out):
             taken[ring].append(tag)
             return psum.tile(shape, F32, name=tag, tag=tag)
 
-        xs = [keep.tile([P, T], F32, name="xs_%d" % g) for g in range(G)]
+        xs = keep.tile([P, G * T], F32, name="xs")
         vb = keep.tile([P, G * T], BF16, name="vb")
         vf = keep.tile([P, G * T], F32, name="vf")
         ident = keep.tile([P, P], F32, name="ident")
-        warm = keep.tile([P, 2], F32, name="warm")
-        left_b = grid("left_b", G, 2, [P, 2, H], U8)
-        right_b = row("right_b", G, [P, T, H], U8)
+        ramp = keep.tile([P, P], I32, name="ramp")
+        xb = grid("xb", G, 2, [P, T, H], U8)
         left_w = row("left_w", G, [P, T, H], BF16)
         left_i = row("left_i", G, [P, H, T], BF16)
         left_c = row("left_c", G, [P, H], U32)
@@ -70,8 +70,7 @@ def tile_loewdin_fock_shift_s7_kernel(tc, f, x_bytes, x_scale, y, v, out):
         fi = grid("fi", G, 2, [P, 2, G * P * T], BF16)
         fc = grid("fc", G, 2, [P, 2 * G * P], U32)
         fk = grid("fk", G, 2, [P, 2 * G * P], U8)
-        left_y = grid("left_y", G, 2, [P, T, Q], BF16)
-        right_y = row("right_y", G, [P, T, H], BF16)
+        ys = grid("ys", G, 2, [P, T, H], BF16)
         vy = grid("vy", G, 4, [P, T, Q], F32)
         hi = row("hi", 4, [P, G, Q, T], BF16)
         hc = row("hc", 4, [P, G, Q], U32)
@@ -79,8 +78,14 @@ def tile_loewdin_fock_shift_s7_kernel(tc, f, x_bytes, x_scale, y, v, out):
 
         copy = {"V": nc.vector.tensor_copy, "S": nc.scalar.copy}
 
+        def load_x(g, h):
+            nc.sync.dma_start(out=xb[g][h][:], in_=x_rows[g][:, :, h * H : (h + 1) * H])
+
         def load_f(g, t):
             nc.sync.dma_start(out=fs[g][t][:], in_=f_rows[g][:, t, :])
+
+        def load_y(g, h):
+            nc.sync.dma_start(out=ys[g][h][:], in_=y_rows[g][:, :, h * H : (h + 1) * H])
 
         def times_column(dst, src, column, eng):
             if eng == "V":
@@ -89,12 +94,11 @@ def tile_loewdin_fock_shift_s7_kernel(tc, f, x_bytes, x_scale, y, v, out):
                 nc.scalar.activation(out=dst, in_=src, func=COPY, scale=column)
 
         def widen_left(g, t, eng):
-            src = left_b[g][t // 2][:, t % 2, :]
-            times_column(left_w[g][:, t, :], src.bitcast(FP8), xs[g][:, t : t + 1], eng)
+            times_column(left_w[g][:, t, :], xb[g][0][:, t, :].bitcast(FP8), xs[:, g * T + t : g * T + t + 1], eng)
 
         def widen_right(q, g, t, eng):
-            src = right_b[g][:, t, (q - 2) * Q : (q - 1) * Q].bitcast(FP8)
-            times_column(right_w[q - 2][:, g, t, :], src, xs[g][:, t : t + 1], eng)
+            src = xb[g][1][:, t, (q - 2) * Q : (q - 1) * Q].bitcast(FP8)
+            times_column(right_w[q - 2][:, g, t, :], src, xs[:, g * T + t : g * T + t + 1], eng)
 
         def quant(mixed, codes, scales):
             nc.vector.quantize_mx(out=codes.bitcast(FP8X4), scales=scales, in_=mixed)
@@ -159,7 +163,7 @@ def tile_loewdin_fock_shift_s7_kernel(tc, f, x_bytes, x_scale, y, v, out):
         def scale_y(q, g, engines):
             for t, eng in enumerate(engines):
                 if eng != "-":
-                    src = left_y[g][q][:, t, :] if q < 2 else right_y[g][:, t, (q - 2) * Q : (q - 1) * Q]
+                    src = ys[g][q // 2][:, t, (q % 2) * Q : (q % 2 + 1) * Q]
                     times_column(vy[g][q][:, t, :], src, vf[:, g * T + t : g * T + t + 1], eng)
 
         half_done = {}
@@ -241,34 +245,28 @@ def tile_loewdin_fock_shift_s7_kernel(tc, f, x_bytes, x_scale, y, v, out):
                 out=out[i0 * P : (i0 + count) * P, j0 : j0 + width].rearrange("(i p) j -> p i j", p=P), in_=res[:]
             )
 
-        scale_rows = x_scale.rearrange("(g p t) o -> g p (t o)", p=P, t=T)
+        nc.scalar.dma_start(out=xs[:], in_=x_scale.rearrange("(g p t) o -> p g (t o)", p=P, t=T))
+        nc.scalar.dma_start(out=vb[:], in_=v.rearrange("(g p t) -> p g t", p=P, t=T))
         for g in range(G):
-            nc.scalar.dma_start(out=xs[g][:], in_=scale_rows[g])
-        for g in range(G):
-            for r in range(2):
-                nc.sync.dma_start(out=left_b[g][r][:], in_=x_rows[g][:, 2 * r : 2 * r + 2, 0:H])
+            load_x(g, 0)
         for g in range(G):
             for t in range(T):
                 load_f(g, t)
+        load_y(0, 0)
+        load_y(1, 0)
         for g in range(G):
-            nc.sync.dma_start(out=left_y[g][0][:], in_=y_rows[g][:, :, 0:Q])
+            load_x(g, 1)
         for g in range(G):
-            nc.sync.dma_start(out=right_b[g][:], in_=x_rows[g][:, :, H:N])
-        for g in range(G):
-            nc.sync.dma_start(out=left_y[g][1][:], in_=y_rows[g][:, :, Q:H])
-        for g in range(G):
-            nc.sync.dma_start(out=right_y[g][:], in_=y_rows[g][:, :, H:N])
+            load_y(g, 1)
 
-        nc.vector.memset(warm[:], 0.0)
-        nc.scalar.activation(out=warm[:, 1:2], in_=warm[:, 0:1], func=COPY)
-        make_identity(nc, ident[:])
+        nc.gpsimd.iota(ramp[:], pattern=[[1, P]], base=0, channel_multiplier=-1)
+        nc.scalar.activation(out=ident[:], in_=ramp[:].bitcast(U32), func=RELU, scale=-1.0, bias=1.0)
 
         for t, eng in enumerate("VSVV"):
             widen_left(0, t, eng)
         for t, eng in enumerate("VSSS"):
             widen_left(1, t, eng)
         lay_left(0)
-        nc.scalar.dma_start(out=vb[:], in_=v.rearrange("(g p t) -> p g t", p=P, t=T))
         lay_left(1)
         quant_left(0)
         for g in range(G):

@@ -36,14 +36,14 @@ def tile_loewdin_fock_shift_s7_kernel(tc, f, x_bytes, x_scale, y, v, out):
         psum = ctx.enter_context(tc.psum_pool(name="psum", bufs=1))
         ctx.enter_context(tc.manual_schedule())
 
+        def tile(name, shape, dtype, tag=None):
+            return keep.tile(shape, dtype, name=name, tag=tag or name, align_bytes=256)
+
         def grid(name, rows, cols, shape, dtype):
-            return [
-                [keep.tile(shape, dtype, name="%s_%d_%d" % (name, a, b), align_bytes=256) for b in range(cols)]
-                for a in range(rows)
-            ]
+            return [[tile("%s_%d_%d" % (name, a, b), shape, dtype) for b in range(cols)] for a in range(rows)]
 
         def row(name, count, shape, dtype):
-            return [keep.tile(shape, dtype, name="%s_%d" % (name, a), align_bytes=256) for a in range(count)]
+            return [tile("%s_%d" % (name, a), shape, dtype) for a in range(count)]
 
         taken = ([], [])
 
@@ -62,19 +62,19 @@ def tile_loewdin_fock_shift_s7_kernel(tc, f, x_bytes, x_scale, y, v, out):
         left_i = row("left_i", G, [P, H, T], BF16)
         left_c = row("left_c", G, [P, H], U32)
         left_k = row("left_k", G, [P, H], U8)
-        right_w = row("right_w", 2, [P, G, T, Q], BF16)
-        right_i = row("right_i", 2, [P, G, Q, T], BF16)
-        right_c = row("right_c", 2, [P, G, Q], U32)
-        right_k = row("right_k", 2, [P, G, Q], U8)
+        right_w = grid("right_w", 2, G, [P, T, Q], BF16)
+        right_i = grid("right_i", 2, G, [P, Q, T], BF16)
+        right_c = grid("right_c", 2, G, [P, Q], U32)
+        right_k = grid("right_k", 2, G, [P, Q], U8)
         fs = grid("fs", G, T, [P, N], BF16)
         fi = grid("fi", G, 2, [P, 2, G * P * T], BF16)
         fc = grid("fc", G, 2, [P, 2 * G * P], U32)
         fk = grid("fk", G, 2, [P, 2 * G * P], U8)
-        ys = grid("ys", G, 2, [P, T, H], BF16)
-        vy = grid("vy", G, 4, [P, T, Q], F32)
         hi = row("hi", 4, [P, G, Q, T], BF16)
         hc = row("hc", 4, [P, G, Q], U32)
         hk = row("hk", 4, [P, G, Q], U8)
+        ys = {}
+        vy = {}
 
         copy = {"V": nc.vector.tensor_copy, "S": nc.scalar.copy}
 
@@ -84,52 +84,57 @@ def tile_loewdin_fock_shift_s7_kernel(tc, f, x_bytes, x_scale, y, v, out):
         def load_f(g, t):
             nc.sync.dma_start(out=fs[g][t][:], in_=f_rows[g][:, t, :])
 
-        def load_y(g, h):
-            nc.sync.dma_start(out=ys[g][h][:], in_=y_rows[g][:, :, h * H : (h + 1) * H])
+        def load_y(g, q0, count):
+            piece = tile("ys_%d_%d" % (g, q0), [P, T, count * Q], BF16)
+            nc.sync.dma_start(out=piece[:], in_=y_rows[g][:, :, q0 * Q : (q0 + count) * Q])
+            ys.update({(g, q0 + i): (piece, i * Q) for i in range(count)})
+
+        def room_vy(g, q0, count, tag=None):
+            piece = tile("vy_%d_%d" % (g, q0), [P, T, count * Q], F32, tag)
+            vy.update({(g, q0 + i): (piece, i * Q) for i in range(count)})
 
         def times_column(dst, src, column, eng):
             if eng == "V":
                 nc.vector.tensor_scalar(out=dst, in0=src, scalar1=column, scalar2=None, op0=MULT)
+            elif eng == "G":
+                nc.gpsimd.tensor_scalar(out=dst, in0=src, scalar1=column, scalar2=1.0, op0=MULT, op1=MULT)
             else:
                 nc.scalar.activation(out=dst, in_=src, func=COPY, scale=column)
 
         def widen_left(g, t, eng):
             times_column(left_w[g][:, t, :], xb[g][0][:, t, :].bitcast(FP8), xs[:, g * T + t : g * T + t + 1], eng)
 
-        def widen_right(q, g, t, eng):
-            src = xb[g][1][:, t, (q - 2) * Q : (q - 1) * Q].bitcast(FP8)
-            times_column(right_w[q - 2][:, g, t, :], src, xs[:, g * T + t : g * T + t + 1], eng)
+        def widen_right(q, g, engines):
+            for t, eng in enumerate(engines):
+                src = xb[g][1][:, t, (q - 2) * Q : (q - 1) * Q].bitcast(FP8)
+                times_column(right_w[q - 2][g][:, t, :], src, xs[:, g * T + t : g * T + t + 1], eng)
 
         def quant(mixed, codes, scales):
             nc.vector.quantize_mx(out=codes.bitcast(FP8X4), scales=scales, in_=mixed)
 
-        def lay_left(g):
+        def lay(mixed, planes):
             nc.vector.tensor_copy(
-                out=left_i[g][:].rearrange("p (c i) t -> p c t i", i=4),
-                in_=left_w[g][:].rearrange("p t (c i) -> p c t i", i=4),
+                out=mixed[:].rearrange("p (c i) t -> p c t i", i=4),
+                in_=planes[:].rearrange("p t (c i) -> p c t i", i=4),
             )
 
-        def lay_right(q):
-            nc.vector.tensor_copy(
-                out=right_i[q - 2][:].rearrange("p g (c i) t -> p g c t i", i=4),
-                in_=right_w[q - 2][:].rearrange("p g t (c i) -> p g c t i", i=4),
-            )
+        def lay_left(g):
+            lay(left_i[g], left_w[g])
+
+        def lay_right(q, g):
+            lay(right_i[q - 2][g], right_w[q - 2][g])
 
         def quant_left(g):
             quant(left_i[g][:].rearrange("p j t -> p (j t)"), left_c[g][:], left_k[g][:])
 
-        def quant_right(q):
-            quant(
-                right_i[q - 2][:].rearrange("p g j t -> p (g j t)"),
-                right_c[q - 2][:].rearrange("p g j -> p (g j)"),
-                right_k[q - 2][:].rearrange("p g j -> p (g j)"),
-            )
+        def quant_right(q, g):
+            quant(right_i[q - 2][g][:].rearrange("p j t -> p (j t)"), right_c[q - 2][g][:], right_k[q - 2][g][:])
 
         def x_operand(g, j0):
             if j0 < H:
                 return left_c[g][:, j0 : j0 + P].bitcast(FP8X4), left_k[g][:, j0 : j0 + P]
             q, lo = divmod(j0 - H, Q)
-            return right_c[q][:, g, lo : lo + P].bitcast(FP8X4), right_k[q][:, g, lo : lo + P]
+            return right_c[q][g][:, lo : lo + P].bitcast(FP8X4), right_k[q][g][:, lo : lo + P]
 
         def quant_h(q):
             quant(
@@ -160,11 +165,12 @@ def tile_loewdin_fock_shift_s7_kernel(tc, f, x_bytes, x_scale, y, v, out):
                 out=fc[g][r][:].bitcast(FP8X4), scales=fk[g][r][:], in_=fi[g][r][:].rearrange("p s k -> p (s k)")
             )
 
-        def scale_y(q, g, engines):
+        def scale_y(q, g, engines, count=1):
+            (src, a), (dst, b) = ys[(g, q)], vy[(g, q)]
             for t, eng in enumerate(engines):
                 if eng != "-":
-                    src = ys[g][q // 2][:, t, (q % 2) * Q : (q % 2 + 1) * Q]
-                    times_column(vy[g][q][:, t, :], src, vf[:, g * T + t : g * T + t + 1], eng)
+                    column = vf[:, g * T + t : g * T + t + 1]
+                    times_column(dst[:, t, b : b + count * Q], src[:, t, a : a + count * Q], column, eng)
 
         half_done = {}
 
@@ -185,12 +191,13 @@ def tile_loewdin_fock_shift_s7_kernel(tc, f, x_bytes, x_scale, y, v, out):
                     )
             half_done[(q, g, n)] = ps
 
-        def h_slot(tile, q, g, n):
+        def h_slot(tiles, q, g, n):
             a, b = (n, g) if q == 3 else (g, n)
-            return tile[q][:, a, b * P : (b + 1) * P]
+            return tiles[q][:, a, b * P : (b + 1) * P]
 
         def shift(q, g, n):
-            addend = vy[g][q][:, :, n * P : (n + 1) * P]
+            piece, lo = vy[(g, q)]
+            addend = piece[:, :, lo + n * P : lo + (n + 1) * P]
             nc.vector.tensor_tensor(
                 out=h_slot(hi, q, g, n).rearrange("p (c i) t -> p c t i", i=4),
                 in0=half_done[(q, g, n)][:].rearrange("p t (c i) -> p c t i", i=4),
@@ -198,9 +205,8 @@ def tile_loewdin_fock_shift_s7_kernel(tc, f, x_bytes, x_scale, y, v, out):
                 op=ADD,
             )
 
-        def quant_last(n):
-            for g in range(G):
-                quant(h_slot(hi, 3, g, n).rearrange("p j t -> p (j t)"), h_slot(hc, 3, g, n), h_slot(hk, 3, g, n))
+        def quant_last(n, g):
+            quant(h_slot(hi, 3, g, n).rearrange("p j t -> p (j t)"), h_slot(hc, 3, g, n), h_slot(hk, 3, g, n))
 
         sums = {}
 
@@ -239,7 +245,7 @@ def tile_loewdin_fock_shift_s7_kernel(tc, f, x_bytes, x_scale, y, v, out):
         def finish(j0, i0, eng):
             ps = sums[(j0, i0)]
             count, width = ps.shape[1], ps.shape[2]
-            res = keep.tile([P, count, width], F32, name="res_%d_%d" % (j0, i0), align_bytes=256)
+            res = tile("res_%d_%d" % (j0, i0), [P, count, width], F32)
             copy[eng](out=res[:], in_=ps[:])
             nc.sync.dma_start(
                 out=out[i0 * P : (i0 + count) * P, j0 : j0 + width].rearrange("(i p) j -> p i j", p=P), in_=res[:]
@@ -252,12 +258,13 @@ def tile_loewdin_fock_shift_s7_kernel(tc, f, x_bytes, x_scale, y, v, out):
         for g in range(G):
             for t in range(T):
                 load_f(g, t)
-        load_y(0, 0)
-        load_y(1, 0)
+        load_y(0, 0, 1)
+        load_y(1, 0, 2)
         for g in range(G):
             load_x(g, 1)
-        for g in range(G):
-            load_y(g, 1)
+        load_y(0, 1, 1)
+        load_y(1, 2, 2)
+        load_y(0, 2, 2)
 
         nc.gpsimd.iota(ramp[:], pattern=[[1, P]], base=0, channel_multiplier=-1)
         nc.scalar.activation(out=ident[:], in_=ramp[:].bitcast(U32), func=RELU, scale=-1.0, bias=1.0)
@@ -278,48 +285,55 @@ def tile_loewdin_fock_shift_s7_kernel(tc, f, x_bytes, x_scale, y, v, out):
         quant_f(0, 1)
         nc.vector.tensor_copy(out=vf[:], in_=vb[:])
         quant_f(1, 0)
-        scale_y(0, 0, "VVSS")
+        for g in range(G):
+            room_vy(g, 0, 1)
+        scale_y(0, 0, "VVVS")
         quant_f(1, 1)
-        scale_y(0, 1, "VVSS")
+        scale_y(0, 1, "SSSS")
+        room_vy(1, 1, 1, "fi_1_1")
+        scale_y(1, 1, "GGGG")
         for q in range(2):
             for g in range(G):
                 for n in range(2):
                     first(q, g, n, q)
         for g in range(G):
-            for t in range(T):
-                widen_right(2, g, t, "S")
+            widen_right(2, g, "SSSS")
         for g in range(G):
             for n in range(2):
                 shift(0, g, n)
-        scale_y(1, 0, "VVSS")
+        lay_right(2, 0)
         quant_h(0)
-        scale_y(1, 1, "SSSS")
-        lay_right(2)
+        lay_right(2, 1)
+        quant_right(2, 0)
+        room_vy(0, 1, 1)
+        scale_y(1, 0, "SSSS")
+        quant_right(2, 1)
+        room_vy(1, 2, 2, "right_i_0_1")
+        scale_y(2, 1, "GG--", 2)
+        widen_right(3, 0, "SSSS")
         for b in range(2):
             second(0, b, 0)
-        shift(1, 0, 0)
-        quant_right(2)
         for b in range(2):
             finish(0, 2 * b, "S")
+        widen_right(3, 1, "SSSS")
         for g in range(G):
-            for t in range(T):
-                widen_right(3, g, t, "S")
-        shift(1, 0, 1)
+            for n in range(2):
+                shift(1, g, n)
         for n in range(2):
             first(2, 0, n, 0)
-        for n in range(2):
-            shift(1, 1, n)
         second(0, 2, 1)
         for n in range(2):
             first(2, 1, n, 0)
-        scale_y(2, 0, "SSS-")
-        finish(0, 4, "S")
+        quant_h_pass(1, 0)
+        quant_h_pass(1, 1)
         for g in range(G):
-            quant_h_pass(1, g)
-        lay_right(3)
-        scale_y(2, 0, "---V")
-        quant_right(3)
-        scale_y(2, 1, "SSSS")
+            lay_right(3, g)
+        for g in range(G):
+            quant_right(3, g)
+        finish(0, 4, "S")
+        room_vy(0, 2, 1)
+        scale_y(2, 0, "SSSS")
+        scale_y(2, 1, "--SS", 2)
         for b in range(3):
             second(1, b, 1)
             finish(Q, 2 * b, "S")
@@ -335,18 +349,20 @@ def tile_loewdin_fock_shift_s7_kernel(tc, f, x_bytes, x_scale, y, v, out):
         first(3, 0, 1, 0)
         for g in range(G):
             quant_h_pass(2, g)
+        room_vy(0, 3, 1)
         scale_y(3, 0, "VVVV")
-        scale_y(3, 1, "VSSS")
         for b in range(4):
             second(2, b, 1)
             finish(2 * Q, 2 * b, "S")
         first(3, 1, 1, 0)
         shift(3, 0, 0)
         shift(3, 1, 0)
-        quant_last(0)
+        quant_last(0, 0)
         shift(3, 0, 1)
+        quant_last(0, 1)
+        quant_last(1, 0)
         shift(3, 1, 1)
-        quant_last(1)
+        quant_last(1, 1)
         for i0 in range(0, 8, 2):
             second_last(0, i0, 2, i0 // 6)
             finish(3 * Q, i0, "SSSV"[i0 // 2])

@@ -22,7 +22,7 @@ G = 2
 T = 4
 H = 512
 Q = 256
-BANKS = 4
+BANKS = 8
 
 
 def tile_loewdin_fock_shift_s7_kernel(tc, f, x_bytes, x_scale, y, v, out):
@@ -45,12 +45,11 @@ def tile_loewdin_fock_shift_s7_kernel(tc, f, x_bytes, x_scale, y, v, out):
         def row(name, count, shape, dtype):
             return [tile("%s_%d" % (name, a), shape, dtype) for a in range(count)]
 
-        taken = ([], [])
+        free = list(range(BANKS))
 
-        def bank(ring, shape):
-            tag = "bank_%d_%d" % (ring, len(taken[ring]) % BANKS)
-            taken[ring].append(tag)
-            return psum.tile(shape, F32, name=tag, tag=tag)
+        def bank(shape):
+            number = free.pop(0)
+            return psum.tile(shape, F32, name="bank_%d" % number, tag="bank_%d" % number), number
 
         xs = keep.tile([P, G * T], F32, name="xs")
         vb = keep.tile([P, G * T], BF16, name="vb")
@@ -148,22 +147,28 @@ def tile_loewdin_fock_shift_s7_kernel(tc, f, x_bytes, x_scale, y, v, out):
 
         turned = {}
 
-        def turn(g, t):
-            ps = bank(g, [P, G, 2, P])
+        def turn(g, t, c0=0, count=G):
+            ps, number = bank([P, count, 2, P])
             words = fs[g][t][:].bitcast(F32)
-            for c in range(G):
+            for c in range(count):
                 for u in range(2):
-                    nc.tensor.transpose(ps[:, c, u, :], words[:, 256 * c + u : 256 * (c + 1) : 2], ident[:])
-            turned[(g, t)] = ps
+                    lo = 256 * (c0 + c)
+                    nc.tensor.transpose(ps[:, c, u, :], words[:, lo + u : lo + 256 : 2], ident[:])
+            turned[(g, t, c0)] = ps, number
 
-        def turn_out(g, t, eng):
-            dst = fi[g][t // 2][:, t % 2, :].bitcast(F32).rearrange("p (c r u) -> p c r u", c=G, u=2)
-            copy[eng](out=dst, in_=turned[(g, t)][:].rearrange("p c u r -> p c r u"))
+        def turn_out(g, t, eng, c0=0):
+            ps, number = turned[(g, t, c0)]
+            count = ps.shape[1]
+            dst = fi[g][t // 2][:, t % 2, c0 * H : (c0 + count) * H].bitcast(F32)
+            copy[eng](out=dst.rearrange("p (c r u) -> p c r u", c=count, u=2), in_=ps[:].rearrange("p c u r -> p c r u"))
+            free.append(number)
 
         def quant_f(g, r):
-            nc.vector.quantize_mx(
-                out=fc[g][r][:].bitcast(FP8X4), scales=fk[g][r][:], in_=fi[g][r][:].rearrange("p s k -> p (s k)")
-            )
+            quant(fi[g][r][:].rearrange("p s k -> p (s k)"), fc[g][r][:], fk[g][r][:])
+
+        def quant_f_lane(g, t):
+            w = slice(t % 2 * Q, (t % 2 + 1) * Q)
+            quant(fi[g][t // 2][:, t % 2, :], fc[g][t // 2][:, w], fk[g][t // 2][:, w])
 
         def scale_y(q, g, engines, count=1):
             (src, a), (dst, b) = ys[(g, q)], vy[(g, q)]
@@ -174,8 +179,8 @@ def tile_loewdin_fock_shift_s7_kernel(tc, f, x_bytes, x_scale, y, v, out):
 
         half_done = {}
 
-        def first(q, g, n, ring):
-            ps = bank(ring, [P, T, P])
+        def first(q, g, n):
+            ps, number = bank([P, T, P])
             for t in range(T):
                 for c in range(G):
                     w = slice(((t % 2) * G + c) * P, ((t % 2) * G + c + 1) * P)
@@ -189,29 +194,31 @@ def tile_loewdin_fock_shift_s7_kernel(tc, f, x_bytes, x_scale, y, v, out):
                         start=(c == 0),
                         stop=(c == G - 1),
                     )
-            half_done[(q, g, n)] = ps
+            half_done[(q, g, n)] = ps, number
 
         def h_slot(tiles, q, g, n):
             a, b = (n, g) if q == 3 else (g, n)
             return tiles[q][:, a, b * P : (b + 1) * P]
 
         def shift(q, g, n):
+            ps, number = half_done[(q, g, n)]
             piece, lo = vy[(g, q)]
             addend = piece[:, :, lo + n * P : lo + (n + 1) * P]
             nc.vector.tensor_tensor(
                 out=h_slot(hi, q, g, n).rearrange("p (c i) t -> p c t i", i=4),
-                in0=half_done[(q, g, n)][:].rearrange("p t (c i) -> p c t i", i=4),
+                in0=ps[:].rearrange("p t (c i) -> p c t i", i=4),
                 in1=addend.rearrange("p t (c i) -> p c t i", i=4),
                 op=ADD,
             )
+            free.append(number)
 
         def quant_last(n, g):
             quant(h_slot(hi, 3, g, n).rearrange("p j t -> p (j t)"), h_slot(hc, 3, g, n), h_slot(hk, 3, g, n))
 
         sums = {}
 
-        def second(q, b, ring):
-            ps = bank(ring, [P, 2, Q])
+        def second(q, b):
+            ps, number = bank([P, 2, Q])
             for n in range(2):
                 for g in range(G):
                     codes, scales = x_operand(g, (2 * b + n) * P)
@@ -224,10 +231,10 @@ def tile_loewdin_fock_shift_s7_kernel(tc, f, x_bytes, x_scale, y, v, out):
                         start=(g == 0),
                         stop=(g == G - 1),
                     )
-            sums[(q * Q, 2 * b)] = ps
+            sums[(q * Q, 2 * b)] = ps, number
 
-        def second_last(n, i0, count, ring):
-            ps = bank(ring, [P, count, P])
+        def second_last(n, i0, count):
+            ps, number = bank([P, count, P])
             for i in range(count):
                 for g in range(G):
                     codes, scales = x_operand(g, (i0 + i) * P)
@@ -240,24 +247,25 @@ def tile_loewdin_fock_shift_s7_kernel(tc, f, x_bytes, x_scale, y, v, out):
                         start=(g == 0),
                         stop=(g == G - 1),
                     )
-            sums[(3 * Q + n * P, i0)] = ps
+            sums[(3 * Q + n * P, i0)] = ps, number
 
         def finish(j0, i0, eng):
-            ps = sums[(j0, i0)]
+            ps, number = sums[(j0, i0)]
             count, width = ps.shape[1], ps.shape[2]
             res = tile("res_%d_%d" % (j0, i0), [P, count, width], F32)
             copy[eng](out=res[:], in_=ps[:])
+            free.append(number)
             nc.sync.dma_start(
                 out=out[i0 * P : (i0 + count) * P, j0 : j0 + width].rearrange("(i p) j -> p i j", p=P), in_=res[:]
             )
 
         nc.scalar.dma_start(out=xs[:], in_=x_scale.rearrange("(g p t) o -> p g (t o)", p=P, t=T))
-        nc.scalar.dma_start(out=vb[:], in_=v.rearrange("(g p t) -> p g t", p=P, t=T))
         for g in range(G):
             load_x(g, 0)
         for g in range(G):
             for t in range(T):
                 load_f(g, t)
+        nc.sync.dma_start(out=vb[:], in_=v.rearrange("(g p t) -> p g t", p=P, t=T))
         load_y(0, 0, 1)
         load_y(1, 0, 2)
         for g in range(G):
@@ -268,6 +276,15 @@ def tile_loewdin_fock_shift_s7_kernel(tc, f, x_bytes, x_scale, y, v, out):
 
         nc.gpsimd.iota(ramp[:], pattern=[[1, P]], base=0, channel_multiplier=-1)
         nc.scalar.activation(out=ident[:], in_=ramp[:].bitcast(U32), func=RELU, scale=-1.0, bias=1.0)
+        zeros = tile("zeros", [P, H], BF16)
+        nc.vector.memset(zeros[:], 0.0)
+        idle, idle_number = bank([P, H])
+
+        def warm_up(count, width):
+            for i in range(count):
+                nc.tensor.matmul(out=idle[:, :width], lhsT=zeros[:, :P], rhs=zeros[:, :width], start=True, stop=True)
+
+        warm_up(6, H)
 
         for t, eng in enumerate("VSVV"):
             widen_left(0, t, eng)
@@ -276,33 +293,38 @@ def tile_loewdin_fock_shift_s7_kernel(tc, f, x_bytes, x_scale, y, v, out):
         lay_left(0)
         lay_left(1)
         quant_left(0)
-        for g in range(G):
-            for t in range(T):
-                turn(g, t)
-                turn_out(g, t, "S")
+        for lane in range(G * T):
+            turn(lane // T, lane % T)
+            turn_out(lane // T, lane % T, "S")
+            if lane in (2, 5):
+                warm_up(1, Q)
+            if lane == 5:
+                free.append(idle_number)
         quant_f(0, 0)
         quant_left(1)
         quant_f(0, 1)
         nc.vector.tensor_copy(out=vf[:], in_=vb[:])
         quant_f(1, 0)
+        quant_f_lane(1, 2)
         for g in range(G):
             room_vy(g, 0, 1)
-        scale_y(0, 0, "VVVS")
-        quant_f(1, 1)
+        scale_y(0, 0, "VVSS")
+        quant_f_lane(1, 3)
         scale_y(0, 1, "SSSS")
         room_vy(1, 1, 1, "fi_1_1")
         scale_y(1, 1, "GGGG")
         for q in range(2):
             for g in range(G):
                 for n in range(2):
-                    first(q, g, n, q)
+                    first(q, g, n)
         for g in range(G):
             widen_right(2, g, "SSSS")
         for g in range(G):
             for n in range(2):
                 shift(0, g, n)
+        quant_h_pass(0, 0)
+        quant_h_pass(0, 1)
         lay_right(2, 0)
-        quant_h(0)
         lay_right(2, 1)
         quant_right(2, 0)
         room_vy(0, 1, 1)
@@ -312,51 +334,54 @@ def tile_loewdin_fock_shift_s7_kernel(tc, f, x_bytes, x_scale, y, v, out):
         scale_y(2, 1, "GG--", 2)
         widen_right(3, 0, "SSSS")
         for b in range(2):
-            second(0, b, 0)
-        for b in range(2):
-            finish(0, 2 * b, "S")
-        widen_right(3, 1, "SSSS")
+            second(0, b)
+        for n in range(2):
+            first(2, 0, n)
         for g in range(G):
             for n in range(2):
                 shift(1, g, n)
+        for b in range(2):
+            finish(0, 2 * b, "S")
+        widen_right(3, 1, "SSSS")
+        second(0, 2)
         for n in range(2):
-            first(2, 0, n, 0)
-        second(0, 2, 1)
-        for n in range(2):
-            first(2, 1, n, 0)
+            first(2, 1, n)
         quant_h_pass(1, 0)
         quant_h_pass(1, 1)
         for g in range(G):
             lay_right(3, g)
         for g in range(G):
             quant_right(3, g)
-        finish(0, 4, "S")
         room_vy(0, 2, 1)
         scale_y(2, 0, "SSSS")
-        scale_y(2, 1, "--SS", 2)
+        finish(0, 4, "S")
+        room_vy(0, 3, 1, "right_i_1_1")
+        scale_y(3, 0, "GGG-")
+        scale_y(2, 1, "--SS")
         for b in range(3):
-            second(1, b, 1)
-            finish(Q, 2 * b, "S")
-        second(0, 3, 1)
-        finish(0, 6, "S")
+            second(1, b)
+        second(0, 3)
         for g in range(G):
             for n in range(2):
                 shift(2, g, n)
-        first(3, 0, 0, 0)
-        second(1, 3, 1)
+        for b in range(3):
+            finish(Q, 2 * b, "S")
+        finish(0, 6, "S")
+        first(3, 0, 0)
+        second(1, 3)
+        first(3, 1, 0)
+        first(3, 0, 1)
         finish(Q, 6, "S")
-        first(3, 1, 0, 0)
-        first(3, 0, 1, 0)
         for g in range(G):
             quant_h_pass(2, g)
-        room_vy(0, 3, 1)
-        scale_y(3, 0, "VVVV")
+        scale_y(3, 0, "---V")
+        scale_y(3, 1, "--VV")
         for b in range(4):
-            second(2, b, 1)
+            second(2, b)
             finish(2 * Q, 2 * b, "S")
-        first(3, 1, 1, 0)
         shift(3, 0, 0)
         shift(3, 1, 0)
+        first(3, 1, 1)
         quant_last(0, 0)
         shift(3, 0, 1)
         quant_last(0, 1)
@@ -364,8 +389,8 @@ def tile_loewdin_fock_shift_s7_kernel(tc, f, x_bytes, x_scale, y, v, out):
         shift(3, 1, 1)
         quant_last(1, 1)
         for i0 in range(0, 8, 2):
-            second_last(0, i0, 2, i0 // 6)
+            second_last(0, i0, 2)
             finish(3 * Q, i0, "SSSV"[i0 // 2])
         for i0 in range(0, 8, 2):
-            second_last(1, i0, 2, 1 - i0 // 6)
+            second_last(1, i0, 2)
             finish(3 * Q + P, i0, "SV"[i0 // 2 % 2])

@@ -205,9 +205,9 @@ def tile_loewdin_fock_shift_s7_kernel(tc, f, x_bytes, x_scale, y, v, out):
             piece, lo = vy[(g, q)]
             addend = piece[:, :, lo + n * P : lo + (n + 1) * P]
             nc.vector.tensor_tensor(
-                out=h_slot(hi, q, g, n).rearrange("p (c i) t -> p c t i", i=4),
-                in0=ps[:].rearrange("p t (c i) -> p c t i", i=4),
-                in1=addend.rearrange("p t (c i) -> p c t i", i=4),
+                out=h_slot(hi, q, g, n).rearrange("p (c i) t -> p c t i", i=2),
+                in0=ps[:].rearrange("p t (c i) -> p c t i", i=2),
+                in1=addend.rearrange("p t (c i) -> p c t i", i=2),
                 op=ADD,
             )
             free.append(number)

@@ -196,6 +196,25 @@ def tile_loewdin_fock_shift_s7_kernel(tc, f, x_bytes, x_scale, y, v, out):
                     )
             half_done[(q, g, n)] = ps, number
 
+        def first_pair(q, g):
+            banks = [bank([P, T, P]) for n in range(2)]
+            for t in range(T):
+                for c in range(G):
+                    w = slice(((t % 2) * G + c) * P, ((t % 2) * G + c + 1) * P)
+                    for n in range(2):
+                        codes, scales = x_operand(c, q * Q + n * P)
+                        nc.tensor.matmul_mx(
+                            out=banks[n][0][:, t, :],
+                            lhsT=fc[g][t // 2][:, w].bitcast(FP8X4),
+                            lhsT_scale=fk[g][t // 2][:, w],
+                            rhs=codes,
+                            rhs_scale=scales,
+                            start=(c == 0),
+                            stop=(c == G - 1),
+                        )
+            for n in range(2):
+                half_done[(q, g, n)] = banks[n]
+
         def h_slot(tiles, q, g, n):
             a, b = (n, g) if q == 3 else (g, n)
             return tiles[q][:, a, b * P : (b + 1) * P]
@@ -276,15 +295,6 @@ def tile_loewdin_fock_shift_s7_kernel(tc, f, x_bytes, x_scale, y, v, out):
 
         nc.gpsimd.iota(ramp[:], pattern=[[1, P]], base=0, channel_multiplier=-1)
         nc.scalar.activation(out=ident[:], in_=ramp[:].bitcast(U32), func=RELU, scale=-1.0, bias=1.0)
-        zeros = tile("zeros", [P, H], BF16)
-        nc.vector.memset(zeros[:], 0.0)
-        idle, idle_number = bank([P, H])
-
-        def warm_up(count, width):
-            for i in range(count):
-                nc.tensor.matmul(out=idle[:, :width], lhsT=zeros[:, :P], rhs=zeros[:, :width], start=True, stop=True)
-
-        warm_up(6, H)
 
         for t, eng in enumerate("VSVV"):
             widen_left(0, t, eng)
@@ -293,13 +303,10 @@ def tile_loewdin_fock_shift_s7_kernel(tc, f, x_bytes, x_scale, y, v, out):
         lay_left(0)
         lay_left(1)
         quant_left(0)
-        for lane in range(G * T):
-            turn(lane // T, lane % T)
-            turn_out(lane // T, lane % T, "S")
-            if lane in (2, 5):
-                warm_up(1, Q)
-            if lane == 5:
-                free.append(idle_number)
+        for g in range(G):
+            for t in range(T):
+                turn(g, t)
+                turn_out(g, t, "S")
         quant_f(0, 0)
         quant_left(1)
         quant_f(0, 1)
@@ -313,10 +320,11 @@ def tile_loewdin_fock_shift_s7_kernel(tc, f, x_bytes, x_scale, y, v, out):
         scale_y(0, 1, "SSSS")
         room_vy(1, 1, 1, "fi_1_1")
         scale_y(1, 1, "GGGG")
-        for q in range(2):
-            for g in range(G):
-                for n in range(2):
-                    first(q, g, n)
+        for g in range(G):
+            for n in range(2):
+                first(0, g, n)
+        for g in range(G):
+            first_pair(1, g)
         for g in range(G):
             widen_right(2, g, "SSSS")
         for g in range(G):
@@ -335,8 +343,7 @@ def tile_loewdin_fock_shift_s7_kernel(tc, f, x_bytes, x_scale, y, v, out):
         widen_right(3, 0, "SSSS")
         for b in range(2):
             second(0, b)
-        for n in range(2):
-            first(2, 0, n)
+        first_pair(2, 0)
         for g in range(G):
             for n in range(2):
                 shift(1, g, n)
@@ -344,8 +351,7 @@ def tile_loewdin_fock_shift_s7_kernel(tc, f, x_bytes, x_scale, y, v, out):
             finish(0, 2 * b, "S")
         widen_right(3, 1, "SSSS")
         second(0, 2)
-        for n in range(2):
-            first(2, 1, n)
+        first_pair(2, 1)
         quant_h_pass(1, 0)
         quant_h_pass(1, 1)
         for g in range(G):

@@ -113,8 +113,8 @@ def tile_loewdin_fock_shift_s7_kernel(tc, f, x_bytes, x_scale, y, v, out):
 
         def lay(mixed, planes):
             nc.vector.tensor_copy(
-                out=mixed[:].rearrange("p (c i) t -> p c t i", i=4),
-                in_=planes[:].rearrange("p t (c i) -> p c t i", i=4),
+                out=mixed[:].rearrange("p (c h i) t -> p h c t i", h=2, i=4),
+                in_=planes[:].rearrange("p t (c h i) -> p h c t i", h=2, i=4),
             )
 
         def lay_left(g):
@@ -234,6 +234,9 @@ def tile_loewdin_fock_shift_s7_kernel(tc, f, x_bytes, x_scale, y, v, out):
         def quant_last(n, g):
             quant(h_slot(hi, 3, g, n).rearrange("p j t -> p (j t)"), h_slot(hc, 3, g, n), h_slot(hk, 3, g, n))
 
+        def quant_chunk(n):
+            quant(hi[3][:, n].rearrange("p j t -> p (j t)"), hc[3][:, n, :], hk[3][:, n, :])
+
         sums = {}
 
         def second(q, b):
@@ -267,6 +270,24 @@ def tile_loewdin_fock_shift_s7_kernel(tc, f, x_bytes, x_scale, y, v, out):
                         stop=(g == G - 1),
                     )
             sums[(3 * Q + n * P, i0)] = ps, number
+
+        def second_last_by_pass(n, starts):
+            banks = {i0: bank([P, 2, P]) for i0 in starts}
+            for g in range(G):
+                for i0 in starts:
+                    for i in range(2):
+                        codes, scales = x_operand(g, (i0 + i) * P)
+                        nc.tensor.matmul_mx(
+                            out=banks[i0][0][:, i, :],
+                            lhsT=codes,
+                            lhsT_scale=scales,
+                            rhs=h_slot(hc, 3, g, n).bitcast(FP8X4),
+                            rhs_scale=h_slot(hk, 3, g, n),
+                            start=(g == 0 and i == 0),
+                            stop=(g == G - 1 and i == 1),
+                        )
+            for i0 in starts:
+                sums[(3 * Q + n * P, i0)] = banks[i0]
 
         def finish(j0, i0, eng):
             ps, number = sums[(j0, i0)]
@@ -306,17 +327,17 @@ def tile_loewdin_fock_shift_s7_kernel(tc, f, x_bytes, x_scale, y, v, out):
         for g in range(G):
             for t in range(T):
                 turn(g, t)
+                if (g, t) == (1, 3):
+                    nc.scalar.copy(out=vf[:], in_=vb[:])
                 turn_out(g, t, "S")
         quant_f(0, 0)
         quant_left(1)
         quant_f(0, 1)
-        nc.vector.tensor_copy(out=vf[:], in_=vb[:])
         quant_f(1, 0)
-        quant_f_lane(1, 2)
         for g in range(G):
             room_vy(g, 0, 1)
         scale_y(0, 0, "VVSS")
-        quant_f_lane(1, 3)
+        quant_f(1, 1)
         scale_y(0, 1, "SSSS")
         room_vy(1, 1, 1, "fi_1_1")
         scale_y(1, 1, "GGGG")
@@ -397,6 +418,8 @@ def tile_loewdin_fock_shift_s7_kernel(tc, f, x_bytes, x_scale, y, v, out):
         for i0 in range(0, 8, 2):
             second_last(0, i0, 2)
             finish(3 * Q, i0, "SSSV"[i0 // 2])
+        second_last_by_pass(1, (0, 2))
         for i0 in range(0, 8, 2):
-            second_last(1, i0, 2)
+            if i0 >= 4:
+                second_last(1, i0, 2)
             finish(3 * Q + P, i0, "SV"[i0 // 2 % 2])

@@ -319,7 +319,7 @@ def tile_loewdin_fock_shift_s7_kernel(tc, f, x_bytes, x_scale, y, v, out):
 
         for t, eng in enumerate("VSVV"):
             widen_left(0, t, eng)
-        for t, eng in enumerate("VSSS"):
+        for t, eng in enumerate("VVSS"):
             widen_left(1, t, eng)
         lay_left(0)
         lay_left(1)
@@ -327,17 +327,17 @@ def tile_loewdin_fock_shift_s7_kernel(tc, f, x_bytes, x_scale, y, v, out):
         for g in range(G):
             for t in range(T):
                 turn(g, t)
-                if (g, t) == (1, 3):
-                    nc.scalar.copy(out=vf[:], in_=vb[:])
                 turn_out(g, t, "S")
         quant_f(0, 0)
         quant_left(1)
         quant_f(0, 1)
+        nc.vector.tensor_copy(out=vf[:], in_=vb[:])
         quant_f(1, 0)
+        quant_f_lane(1, 2)
         for g in range(G):
             room_vy(g, 0, 1)
-        scale_y(0, 0, "VVSS")
-        quant_f(1, 1)
+        scale_y(0, 0, "VVVS")
+        quant_f_lane(1, 3)
         scale_y(0, 1, "SSSS")
         room_vy(1, 1, 1, "fi_1_1")
         scale_y(1, 1, "GGGG")

from contextlib import ExitStack

import concourse.mybir as mybir

N = 1024
FLOPS = 2 * 2 * N * N * N

F32 = mybir.dt.float32
BF16 = mybir.dt.bfloat16
U32 = mybir.dt.uint32
I32 = mybir.dt.int32
U8 = mybir.dt.uint8
FP8 = mybir.dt.float8_e4m3fn
FP8X4 = mybir.dt.float8_e4m3fn_x4
COPY = mybir.ActivationFunctionType.Copy
RELU = mybir.ActivationFunctionType.Relu
MULT = mybir.AluOpType.mult
ADD = mybir.AluOpType.add

P = 128
G = 2
T = 4
H = 512
Q = 256
BANKS = 8


def tile_loewdin_fock_shift_s7_kernel(tc, f, x_bytes, x_scale, y, v, out):
    nc = tc.nc
    x_rows = x_bytes.rearrange("(g p t) j -> g p t j", p=P, t=T)
    f_rows = f.rearrange("(g p t) b -> g p t b", p=P, t=T)
    y_rows = y.rearrange("(g p t) j -> g p t j", p=P, t=T)

    with ExitStack() as ctx:
        keep = ctx.enter_context(tc.tile_pool(name="keep", bufs=1))
        psum = ctx.enter_context(tc.psum_pool(name="psum", bufs=1))
        ctx.enter_context(tc.manual_schedule())

        def tile(name, shape, dtype, tag=None):
            return keep.tile(shape, dtype, name=name, tag=tag or name, align_bytes=256)

        def grid(name, rows, cols, shape, dtype):
            return [[tile("%s_%d_%d" % (name, a, b), shape, dtype) for b in range(cols)] for a in range(rows)]

        def row(name, count, shape, dtype):
            return [tile("%s_%d" % (name, a), shape, dtype) for a in range(count)]

        free = list(range(BANKS))

        def bank(shape):
            number = free.pop(0)
            return psum.tile(shape, F32, name="bank_%d" % number, tag="bank_%d" % number), number

        xs = keep.tile([P, G * T], F32, name="xs")
        vb = keep.tile([P, G * T], BF16, name="vb")
        vf = keep.tile([P, G * T], F32, name="vf")
        ident = keep.tile([P, P], F32, name="ident")
        ramp = keep.tile([P, P], I32, name="ramp")
        xb = grid("xb", G, 2, [P, T, H], U8)
        left_w = row("left_w", G, [P, T, H], BF16)
        left_i = row("left_i", G, [P, H, T], BF16)
        left_c = row("left_c", G, [P, H], U32)
        left_k = row("left_k", G, [P, H], U8)
        right_w = grid("right_w", 2, G, [P, T, Q], BF16)
        right_i = grid("right_i", 2, G, [P, Q, T], BF16)
        right_c = grid("right_c", 2, G, [P, Q], U32)
        right_k = grid("right_k", 2, G, [P, Q], U8)
        fs = grid("fs", G, T, [P, N], BF16)
        fi = grid("fi", G, 2, [P, 2, G * P * T], BF16)
        fc = grid("fc", G, 2, [P, 2 * G * P], U32)
        fk = grid("fk", G, 2, [P, 2 * G * P], U8)
        hi = row("hi", 4, [P, G, Q, T], BF16)
        hc = row("hc", 4, [P, G, Q], U32)
        hk = row("hk", 4, [P, G, Q], U8)
        ys = {}
        vy = {}

        copy = {"V": nc.vector.tensor_copy, "S": nc.scalar.copy}

        def load_x(g, h):
            nc.sync.dma_start(out=xb[g][h][:], in_=x_rows[g][:, :, h * H : (h + 1) * H])

        def load_f(g, t):
            nc.sync.dma_start(out=fs[g][t][:], in_=f_rows[g][:, t, :])

        def load_y(g, q0, count):
            piece = tile("ys_%d_%d" % (g, q0), [P, T, count * Q], BF16)
            nc.sync.dma_start(out=piece[:], in_=y_rows[g][:, :, q0 * Q : (q0 + count) * Q])
            ys.update({(g, q0 + i): (piece, i * Q) for i in range(count)})

        def room_vy(g, q0, count, tag=None):
            piece = tile("vy_%d_%d" % (g, q0), [P, T, count * Q], F32, tag)
            vy.update({(g, q0 + i): (piece, i * Q) for i in range(count)})

        def times_column(dst, src, column, eng):
            if eng == "V":
                nc.vector.tensor_scalar(out=dst, in0=src, scalar1=column, scalar2=None, op0=MULT)
            elif eng == "G":
                nc.gpsimd.tensor_scalar(out=dst, in0=src, scalar1=column, scalar2=1.0, op0=MULT, op1=MULT)
            else:
                nc.scalar.activation(out=dst, in_=src, func=COPY, scale=column)

        def widen_left(g, t, eng):
            times_column(left_w[g][:, t, :], xb[g][0][:, t, :].bitcast(FP8), xs[:, g * T + t : g * T + t + 1], eng)

        def widen_right(q, g, engines):
            for t, eng in enumerate(engines):
                src = xb[g][1][:, t, (q - 2) * Q : (q - 1) * Q].bitcast(FP8)
                times_column(right_w[q - 2][g][:, t, :], src, xs[:, g * T + t : g * T + t + 1], eng)

        def quant(mixed, codes, scales):
            nc.vector.quantize_mx(out=codes.bitcast(FP8X4), scales=scales, in_=mixed)

        def lay(mixed, planes):
            nc.vector.tensor_copy(
                out=mixed[:].rearrange("p (c h i) t -> p h c t i", h=2, i=4),
                in_=planes[:].rearrange("p t (c h i) -> p h c t i", h=2, i=4),
            )

        def lay_left(g):
            lay(left_i[g], left_w[g])

        def lay_right(q, g):
            lay(right_i[q - 2][g], right_w[q - 2][g])

        def quant_left(g):
            quant(left_i[g][:].rearrange("p j t -> p (j t)"), left_c[g][:], left_k[g][:])

        def quant_right(q, g):
            quant(right_i[q - 2][g][:].rearrange("p j t -> p (j t)"), right_c[q - 2][g][:], right_k[q - 2][g][:])

        def x_operand(g, j0):
            if j0 < H:
                return left_c[g][:, j0 : j0 + P].bitcast(FP8X4), left_k[g][:, j0 : j0 + P]
            q, lo = divmod(j0 - H, Q)
            return right_c[q][g][:, lo : lo + P].bitcast(FP8X4), right_k[q][g][:, lo : lo + P]

        def quant_h(q):
            quant(
                hi[q][:].rearrange("p g j t -> p (g j t)"),
                hc[q][:].rearrange("p g j -> p (g j)"),
                hk[q][:].rearrange("p g j -> p (g j)"),
            )

        def quant_h_pass(q, g):
            quant(hi[q][:, g].rearrange("p j t -> p (j t)"), hc[q][:, g, :], hk[q][:, g, :])

        turned = {}

        def turn(g, t, c0=0, count=G):
            ps, number = bank([P, count, 2, P])
            words = fs[g][t][:].bitcast(F32)
            for c in range(count):
                for u in range(2):
                    lo = 256 * (c0 + c)
                    nc.tensor.transpose(ps[:, c, u, :], words[:, lo + u : lo + 256 : 2], ident[:])
            turned[(g, t, c0)] = ps, number

        def turn_out(g, t, eng, c0=0):
            ps, number = turned[(g, t, c0)]
            count = ps.shape[1]
            dst = fi[g][t // 2][:, t % 2, c0 * H : (c0 + count) * H].bitcast(F32)
            copy[eng](out=dst.rearrange("p (c r u) -> p c r u", c=count, u=2), in_=ps[:].rearrange("p c u r -> p c r u"))
            free.append(number)

        def quant_f(g, r):
            quant(fi[g][r][:].rearrange("p s k -> p (s k)"), fc[g][r][:], fk[g][r][:])

        def quant_f_lane(g, t):
            w = slice(t % 2 * Q, (t % 2 + 1) * Q)
            quant(fi[g][t // 2][:, t % 2, :], fc[g][t // 2][:, w], fk[g][t // 2][:, w])

        def scale_y(q, g, engines, count=1):
            (src, a), (dst, b) = ys[(g, q)], vy[(g, q)]
            for t, eng in enumerate(engines):
                if eng != "-":
                    column = vf[:, g * T + t : g * T + t + 1]
                    times_column(dst[:, t, b : b + count * Q], src[:, t, a : a + count * Q], column, eng)

        half_done = {}

        def first(q, g, n):
            ps, number = bank([P, T, P])
            for t in range(T):
                for c in range(G):
                    w = slice(((t % 2) * G + c) * P, ((t % 2) * G + c + 1) * P)
                    codes, scales = x_operand(c, q * Q + n * P)
                    nc.tensor.matmul_mx(
                        out=ps[:, t, :],
                        lhsT=fc[g][t // 2][:, w].bitcast(FP8X4),
                        lhsT_scale=fk[g][t // 2][:, w],
                        rhs=codes,
                        rhs_scale=scales,
                        start=(c == 0),
                        stop=(c == G - 1),
                    )
            half_done[(q, g, n)] = ps, number

        def first_pair(q, g):
            banks = [bank([P, T, P]) for n in range(2)]
            for t in range(T):
                for c in range(G):
                    w = slice(((t % 2) * G + c) * P, ((t % 2) * G + c + 1) * P)
                    for n in range(2):
                        codes, scales = x_operand(c, q * Q + n * P)
                        nc.tensor.matmul_mx(
                            out=banks[n][0][:, t, :],
                            lhsT=fc[g][t // 2][:, w].bitcast(FP8X4),
                            lhsT_scale=fk[g][t // 2][:, w],
                            rhs=codes,
                            rhs_scale=scales,
                            start=(c == 0),
                            stop=(c == G - 1),
                        )
            for n in range(2):
                half_done[(q, g, n)] = banks[n]

        def h_slot(tiles, q, g, n):
            a, b = (n, g) if q == 3 else (g, n)
            return tiles[q][:, a, b * P : (b + 1) * P]

        def shift(q, g, n):
            ps, number = half_done[(q, g, n)]
            piece, lo = vy[(g, q)]
            addend = piece[:, :, lo + n * P : lo + (n + 1) * P]
            nc.vector.tensor_tensor(
                out=h_slot(hi, q, g, n).rearrange("p (c i) t -> p c t i", i=2),
                in0=ps[:].rearrange("p t (c i) -> p c t i", i=2),
                in1=addend.rearrange("p t (c i) -> p c t i", i=2),
                op=ADD,
            )
            free.append(number)

        def quant_last(n, g):
            quant(h_slot(hi, 3, g, n).rearrange("p j t -> p (j t)"), h_slot(hc, 3, g, n), h_slot(hk, 3, g, n))

        def quant_chunk(n):
            quant(hi[3][:, n].rearrange("p j t -> p (j t)"), hc[3][:, n, :], hk[3][:, n, :])

        sums = {}

        def second(q, b):
            ps, number = bank([P, 2, Q])
            for n in range(2):
                for g in range(G):
                    codes, scales = x_operand(g, (2 * b + n) * P)
                    nc.tensor.matmul_mx(
                        out=ps[:, n, :],
                        lhsT=codes,
                        lhsT_scale=scales,
                        rhs=hc[q][:, g, :].bitcast(FP8X4),
                        rhs_scale=hk[q][:, g, :],
                        start=(g == 0),
                        stop=(g == G - 1),
                    )
            sums[(q * Q, 2 * b)] = ps, number

        def second_last(n, i0, count):
            ps, number = bank([P, count, P])
            for i in range(count):
                for g in range(G):
                    codes, scales = x_operand(g, (i0 + i) * P)
                    nc.tensor.matmul_mx(
                        out=ps[:, i, :],
                        lhsT=codes,
                        lhsT_scale=scales,
                        rhs=h_slot(hc, 3, g, n).bitcast(FP8X4),
                        rhs_scale=h_slot(hk, 3, g, n),
                        start=(g == 0),
                        stop=(g == G - 1),
                    )
            sums[(3 * Q + n * P, i0)] = ps, number

        def second_last_by_pass(n, starts):
            banks = {i0: bank([P, 2, P]) for i0 in starts}
            for g in range(G):
                for i0 in starts:
                    for i in range(2):
                        codes, scales = x_operand(g, (i0 + i) * P)
                        nc.tensor.matmul_mx(
                            out=banks[i0][0][:, i, :],
                            lhsT=codes,
                            lhsT_scale=scales,
                            rhs=h_slot(hc, 3, g, n).bitcast(FP8X4),
                            rhs_scale=h_slot(hk, 3, g, n),
                            start=(g == 0 and i == 0),
                            stop=(g == G - 1 and i == 1),
                        )
            for i0 in starts:
                sums[(3 * Q + n * P, i0)] = banks[i0]

        def finish(j0, i0, eng):
            ps, number = sums[(j0, i0)]
            count, width = ps.shape[1], ps.shape[2]
            res = tile("res_%d_%d" % (j0, i0), [P, count, width], F32)
            copy[eng](out=res[:], in_=ps[:])
            free.append(number)
            nc.sync.dma_start(
                out=out[i0 * P : (i0 + count) * P, j0 : j0 + width].rearrange("(i p) j -> p i j", p=P), in_=res[:]
            )

        nc.scalar.dma_start(out=xs[:], in_=x_scale.rearrange("(g p t) o -> p g (t o)", p=P, t=T))
        for g in range(G):
            load_x(g, 0)
        for g in range(G):
            for t in range(T):
                load_f(g, t)
        nc.sync.dma_start(out=vb[:], in_=v.rearrange("(g p t) -> p g t", p=P, t=T))
        load_y(0, 0, 1)
        load_y(1, 0, 2)
        for g in range(G):
            load_x(g, 1)
        load_y(0, 1, 1)
        load_y(1, 2, 2)
        load_y(0, 2, 2)

        nc.gpsimd.iota(ramp[:], pattern=[[1, P]], base=0, channel_multiplier=-1)
        nc.scalar.activation(out=ident[:], in_=ramp[:].bitcast(U32), func=RELU, scale=-1.0, bias=1.0)

        for t, eng in enumerate("VSVV"):
            widen_left(0, t, eng)
        for t, eng in enumerate("VVSS"):
            widen_left(1, t, eng)
        lay_left(0)
        lay_left(1)
        quant_left(0)
        for g in range(G):
            for t in range(T):
                turn(g, t)
                turn_out(g, t, "S")
        quant_f(0, 0)
        quant_left(1)
        quant_f(0, 1)
        nc.vector.tensor_copy(out=vf[:], in_=vb[:])
        quant_f(1, 0)
        quant_f_lane(1, 2)
        for g in range(G):
            room_vy(g, 0, 1)
        scale_y(0, 0, "VVVS")
        quant_f_lane(1, 3)
        scale_y(0, 1, "SSSS")
        room_vy(1, 1, 1, "fi_1_1")
        scale_y(1, 1, "GGGG")
        for g in range(G):
            for n in range(2):
                first(0, g, n)
        for g in range(G):
            first_pair(1, g)
        for g in range(G):
            widen_right(2, g, "SSSS")
        for g in range(G):
            for n in range(2):
                shift(0, g, n)
        quant_h_pass(0, 0)
        quant_h_pass(0, 1)
        lay_right(2, 0)
        lay_right(2, 1)
        quant_right(2, 0)
        room_vy(0, 1, 1)
        scale_y(1, 0, "SSSS")
        quant_right(2, 1)
        room_vy(1, 2, 2, "right_i_0_1")
        scale_y(2, 1, "GG--", 2)
        widen_right(3, 0, "SSSS")
        for b in range(2):
            second(0, b)
        first_pair(2, 0)
        for g in range(G):
            for n in range(2):
                shift(1, g, n)
        for b in range(2):
            finish(0, 2 * b, "S")
        widen_right(3, 1, "SSSS")
        second(0, 2)
        first_pair(2, 1)
        quant_h_pass(1, 0)
        quant_h_pass(1, 1)
        for g in range(G):
            lay_right(3, g)
        for g in range(G):
            quant_right(3, g)
        room_vy(0, 2, 1)
        scale_y(2, 0, "SSSS")
        finish(0, 4, "S")
        room_vy(0, 3, 1, "right_i_1_1")
        scale_y(3, 0, "GGG-")
        scale_y(2, 1, "--SS")
        for b in range(3):
            second(1, b)
        second(0, 3)
        for g in range(G):
            for n in range(2):
                shift(2, g, n)
        for b in range(3):
            finish(Q, 2 * b, "S")
        finish(0, 6, "S")
        first(3, 0, 0)
        second(1, 3)
        first(3, 1, 0)
        first(3, 0, 1)
        finish(Q, 6, "S")
        for g in range(G):
            quant_h_pass(2, g)
        scale_y(3, 0, "---V")
        scale_y(3, 1, "--VV")
        for b in range(4):
            second(2, b)
            finish(2 * Q, 2 * b, "S")
        shift(3, 0, 0)
        shift(3, 1, 0)
        first(3, 1, 1)
        quant_last(0, 0)
        shift(3, 0, 1)
        quant_last(0, 1)
        quant_last(1, 0)
        shift(3, 1, 1)
        quant_last(1, 1)
        for i0 in range(0, 8, 2):
            second_last(0, i0, 2)
            finish(3 * Q, i0, "SSSV"[i0 // 2])
        second_last_by_pass(1, (0, 2))
        for i0 in range(0, 8, 2):
            if i0 >= 4:
                second_last(1, i0, 2)
            finish(3 * Q + P, i0, "SV"[i0 // 2 % 2])
